import numpy as np
import ml_dtypes


def mxq(x, axis, fmt="e4m3"):
    dtype, down = {"e4m3": (ml_dtypes.float8_e4m3fn, 7), "e5m2": (ml_dtypes.float8_e5m2, 14)}[fmt]
    v = np.moveaxis(np.asarray(x, np.float32).astype(ml_dtypes.bfloat16).astype(np.float64), axis, -1)
    blocks = v.reshape(v.shape[:-1] + (-1, 32))
    amax = np.abs(blocks).max(-1, keepdims=True)
    byte = np.maximum(np.where(amax > 0, np.frexp(amax)[1] - 1 + 127, 0) - down, 1)
    scale = np.exp2(byte - 127.0)
    codes = (blocks / scale).astype(np.float32).astype(dtype).astype(np.float64)
    return np.moveaxis((codes * scale).reshape(v.shape), -1, axis)


WIDE = False


def mx_kscale(k):
    if not WIDE:
        return np.ones(k)
    levels = np.array([10, -10, 5, -5, 0])
    if k % 512:
        return np.exp2(np.random.permutation(np.resize(levels, k // 32))).repeat(32)
    a = np.empty((k // 512, 16))
    for p in range(k // 512):
        a[p, :8] = np.random.permutation(np.resize(levels, 8))
        for g in range(8):
            far = levels[np.abs(levels - a[p, g]) >= 10]
            a[p, g + 8] = far[np.random.randint(len(far))]
    return np.exp2(a.ravel()).repeat(32)


BF16 = ml_dtypes.bfloat16


def bf(x):
    return np.asarray(x, np.float32).astype(BF16)


def f64(x):
    return np.asarray(x).astype(np.float64)

def planes(Y):
    n, m = Y.shape
    b = f64(bf(Y)).reshape(n // 32, 32, m)
    amax = np.abs(b).max(1)
    byte = np.clip(np.where(amax > 0, np.frexp(amax)[1] - 1 + 127 - 7, 1), 1, 254)
    codes = (b * np.exp2(127.0 - byte)[:, None, :]).reshape(n, m).astype(np.float32).astype(ml_dtypes.float8_e4m3fn).view(np.uint8)
    words = codes.reshape(n // 512, 128, 4, m).transpose(0, 1, 3, 2)
    return np.ascontiguousarray(words), np.ascontiguousarray(byte.astype(np.uint8).reshape(n // 512, 16, m))


S, N, M = 1024, 1024, 512


def setup_inputs():
    s = mx_kscale(N)
    t = mx_kscale(M)
    u = mx_kscale(S)
    x = np.random.standard_normal((S, N))
    y = np.random.standard_normal((S, M))
    p = 1.0 + 0.2 * np.random.standard_normal(N)
    c = np.random.standard_normal((M, N)) / np.sqrt(N)
    k = 0.7 * np.random.standard_normal((M, N)) / np.sqrt(M)
    a = np.random.standard_normal((S, S)) / np.sqrt(S)
    g = 1.0 + 0.2 * np.random.standard_normal(S)
    return {"x": bf(x), "y": bf(y * t[None, :]), "p": bf(p * s),
            "c": bf(c * t[:, None] / s[None, :]), "k": bf(k / t[:, None]),
            "a": bf(a / u[None, :]), "g": bf(g * u)}


def innovation(x, y, p, c):
    return y - (mxq(x * p[None, :], 1, "e4m3") @ mxq(c, 1, "e4m3").T)


def core(x, y, p, c, k, a, g):
    x, y, p, c, k, a, g = f64(x), f64(y), f64(p), f64(c), f64(k), f64(a), f64(g)
    nu = innovation(x, y, p, c)
    corr = mxq(nu, 1, "e4m3") @ mxq(k, 0, "e4m3")
    nb = mxq(a, 1, "e4m3") @ mxq(x * g[:, None], 0, "e4m3")
    deg = np.sum(a * g[None, :], axis=1)
    xn = x + corr + 0.5 * (nb - deg[:, None] * x)
    return xn


def reference(x, y, p, c, k, a, g):
    R_out = core(x, y, p, c, k, a, g)
    words, scales = planes(R_out.T)
    return R_out, words, scales

@@ -1,0 +1,426 @@
+from contextlib import ExitStack
+
+import concourse.mybir as mybir
+from concourse.masks import make_identity
+
+S, N, M = 1024, 1024, 512
+FLOPS = 2 * S * N * M + 2 * S * M * N + 2 * S * S * N
+
+F32 = mybir.dt.float32
+BF16 = mybir.dt.bfloat16
+U32 = mybir.dt.uint32
+I32 = mybir.dt.int32
+U8 = mybir.dt.uint8
+FP8X4 = mybir.dt.float8_e4m3fn_x4
+MULT = mybir.AluOpType.mult
+ADD = mybir.AluOpType.add
+SUB = mybir.AluOpType.subtract
+
+P = 128
+KENG = "vg"
+ORDER = "tx01 mu01 mu00 tx00 xp01 tx11 xp00 tx10 xp11 tc00 qx0 tc01 ec00 xp10 tc10 ec01 mu03 mu02 tc11 ec10 qx1 tx21 ec11 qc0 tx20 il000 qc1 tx31 mu13 m1_1 mu10 il001 mu12 m1_0 mu11 nu1 m1_3 il100 nu0 m1_2 xp20 tn0 xp21 il101 ta1 ki00 ta0 ki01 ea1 qx2 ea0 tx30 ki10 en0 nu3 ta3 nu2 ta2 ea3 ki11 qg10 dg0 ea2 qk0 m1_4 il111 qg00 m1_5 xp30 tn1 ta4 xp31 en1 ta5 qn0 ea4 qa0 dd0 dg1 qx3 ea5 m2_00 qa1 il010 nu5 ta6 nu4 il011 qa2 m2_10 qn1 st00 m1_6 ea6 dd1 qa3 m1_7 st10 rd00 m2_20 nu6 il110 nu7 tn2 qa4 ta7 en2 st20 tn3 ea7 qa5 dg2 qn2 rd10 qa6 m2_30 dd2 qa7 en3 qg11 m2_40 rd20 st30 dg3 qn3 rd30 st40 m2_50 dd3 qg01 rd40 m2_60 st50 qk1 to00 rd50 to10 st60 eo00 m2_70 eo10 m2_01 st70 rd60 qo00 m2_11 rd70 st01 to20 st11 to30 rd01 m2_21 eo20 eo30 m2_31 st21 rd11 qo10 m2_41 rd21 st31 m2_51 st41 rd31 to01 rd41 st51 to11 eo01 m2_61 eo11 m2_71 rd51 st61 qo01 to21 rd61 st71 eo21 rd71 to31 eo31 qo11"
+
+
+def tile_signedkalmanconsensusfilterstep_x1_kernel(tc, x, y, p, c, k, a, g, out_0, out_1, out_2):
+    nc = tc.nc
+    with ExitStack() as ctx:
+        keep = ctx.enter_context(tc.tile_pool(name="keep", bufs=1))
+        ring = ctx.enter_context(tc.tile_pool(name="ring", bufs=2))
+        psum_t = ctx.enter_context(tc.psum_pool(name="psum_t", bufs=4))
+        psum_o = ctx.enter_context(tc.psum_pool(name="psum_o", bufs=4))
+
+        def kt(name, shape, dtype):
+            return keep.tile(shape, dtype, name=name, align_bytes=64)
+
+        ident = kt("ident", [P, P], F32)
+        p_t = kt("p_t", [P, 2, 4], BF16)
+        g_t = kt("g_t", [P, 2, 4], BF16)
+        hg = kt("hg", [P, 2, 4], BF16)
+        dd = kt("dd", [P, 8], F32)
+        x_sb = [kt("x_sb%d" % i, [P, 4, N], BF16) for i in range(2)]
+        a_sb = [kt("a_sb%d" % i, [P, 4, S], BF16) for i in range(2)]
+        y_sb = [kt("y_sb%d" % i, [P, 4, M], BF16) for i in range(2)]
+        c_sb = kt("c_sb", [P, 4, N], BF16)
+        k_sb = kt("k_sb", [P, 4, N], BF16)
+        c_t = kt("c_t", [P, 2, M, 4], BF16)
+        c_q = kt("c_q", [P, 2, M], U32)
+        c_s = kt("c_s", [P, 2, M], U8)
+        k_i = kt("k_i", [P, N, 4], BF16)
+        k_q = kt("k_q", [P, N], U32)
+        k_s = kt("k_s", [P, N], U8)
+        xm = [kt("xm%d" % i, [P, 4, N], BF16) for i in range(2)]
+        g_q = [kt("g_q%d" % i, [P, N], U32) for i in range(2)]
+        g_s = [kt("g_s%d" % i, [P, N], U8) for i in range(2)]
+        x_q = [kt("x_q%d" % i, [P, 2, 256], U32) for i in range(4)]
+        x_s = [kt("x_s%d" % i, [P, 2, 256], U8) for i in range(4)]
+        n_q = [kt("n_q%d" % i, [P, 256], U32) for i in range(4)]
+        n_s = [kt("n_s%d" % i, [P, 256], U8) for i in range(4)]
+        a_q = [kt("a_q%d" % i, [P, 2, P], U32) for i in range(8)]
+        a_s = [kt("a_s%d" % i, [P, 2, P], U8) for i in range(8)]
+        o_q = [[kt("o_q%d%d" % (i, j), [P, M], U32) for j in range(2)] for i in range(2)]
+        o_s = [[kt("o_s%d%d" % (i, j), [P, M], U8) for j in range(2)] for i in range(2)]
+        o_t = [[kt("o_t%d%d" % (i, 0), [P, 512, 4], BF16) for i in range(2)]] * 2
+
+        nc.scalar.dma_start(out=p_t[:], in_=p.rearrange("(h q t) -> q h t", h=2, t=4))
+        nc.scalar.dma_start(out=g_t[:], in_=g.rearrange("(h q t) -> q h t", h=2, t=4))
+        make_identity(nc, ident[:])
+        xr = x.rearrange("(g p t) n -> g p t n", g=2, t=4)
+        ar = a.rearrange("(g p t) n -> g p t n", g=2, t=4)
+        yr = y.rearrange("(g p t) n -> g p t n", g=2, t=4)
+        cr = c.rearrange("(b p) n -> p b n", p=P)
+        kr = k.rearrange("(p t) n -> p t n", t=4)
+
+        def ld(dst, src, i, hf):
+            nc.sync.dma_start(out=dst[i][:, 2 * hf : 2 * hf + 2, :], in_=src[i, :, 2 * hf : 2 * hf + 2, :])
+
+        ld(x_sb, xr, 0, 0)
+        ld(x_sb, xr, 0, 1)
+        for b in range(2):
+            nc.sync.dma_start(out=c_sb[:, 2 * b : 2 * b + 2, :], in_=cr[:, 2 * b : 2 * b + 2, :])
+        ld(x_sb, xr, 1, 0)
+        ld(x_sb, xr, 1, 1)
+        nc.sync.dma_start(out=y_sb[0][:], in_=yr[0])
+        nc.sync.dma_start(out=k_sb[:, :, 0:512], in_=kr[:, :, 0:512])
+        ld(a_sb, ar, 0, 0)
+        ld(a_sb, ar, 0, 1)
+        nc.sync.dma_start(out=k_sb[:, :, 512:1024], in_=kr[:, :, 512:1024])
+        ld(a_sb, ar, 1, 0)
+        nc.sync.dma_start(out=y_sb[1][:], in_=yr[1])
+        ld(a_sb, ar, 1, 1)
+        nc.vector.tensor_scalar_mul(hg[:], g_t[:], 0.5)
+
+        st = {}
+
+        def words(t2d):
+            return t2d.bitcast(F32)
+
+        def tx(pi, ng):
+            gi, hf = divmod(pi, 2)
+            if True:
+                ps = psum_t.tile([P, 512], F32, name="tp")
+                for u in range(2):
+                    for j in range(2):
+                        w = words(x_sb[gi][:, 2 * hf + j, :])
+                        nc.tensor.transpose(
+                            ps[:, 256 * u + 128 * j : 256 * u + 128 * j + 128],
+                            w[:, 256 * ng + u : 256 * (ng + 1) : 2],
+                            ident[:],
+                        )
+                st["tx", pi, ng] = ps
+
+        def xp(pi, ng):
+            if ("xt", pi) not in st:
+                xt = ring.tile([P, 2, 1024], BF16, name="xt", align_bytes=64, bufs=3)
+                st["xt", pi] = xt
+            xt = st["xt", pi]
+            if True:
+                ps = st["tx", pi, ng]
+                nc.vector.tensor_tensor(
+                    out=xt[:, ng, :].rearrange("p (s u e) -> p s u e", u=2, e=2),
+                    in0=ps[:].bitcast(BF16).rearrange("p (u s e) -> p s u e", u=2, e=2),
+                    in1=p_t[:, ng, :].rearrange("p (u e) -> p u e", e=2).unsqueeze(1).broadcast_to([P, 256, 2, 2]),
+                    op=MULT,
+                )
+
+        def qx(pi):
+            nc.vector.quantize_mx(
+                out=x_q[pi][:].rearrange("p a b -> p (a b)").bitcast(FP8X4),
+                scales=x_s[pi][:].rearrange("p a b -> p (a b)"),
+                in_=st["xt", pi][:].rearrange("p a b -> p (a b)"),
+            )
+
+        def tcc(b, ng):
+            if True:
+                ps = psum_t.tile([P, 512], F32, name="tp")
+                for u in range(2):
+                    for j in range(2):
+                        w = words(c_sb[:, 2 * b + j, :])
+                        nc.tensor.transpose(
+                            ps[:, 256 * u + 128 * j : 256 * u + 128 * j + 128],
+                            w[:, 256 * ng + u : 256 * (ng + 1) : 2],
+                            ident[:],
+                        )
+                st["tc", b, ng] = ps
+
+        def ec(b, ng):
+            nc.scalar.copy(
+                out=c_t[:, ng, 256 * b : 256 * b + 256, :].rearrange("p m t -> p (m t)").bitcast(F32).rearrange("p (m u) -> p m u", u=2),
+                in_=st["tc", b, ng][:].rearrange("p (u m) -> p m u", u=2),
+            )
+
+        def qc(ng):
+            nc.vector.quantize_mx(
+                out=c_q[:, ng, :].bitcast(FP8X4), scales=c_s[:, ng, :],
+                in_=c_t[:, ng, :, :].rearrange("p m t -> p (m t)"),
+            )
+
+        def mu(gi, t):
+            nc.vector.tensor_scalar_mul(xm[gi][:, t, :], x_sb[gi][:, t, :], hg[:, gi, t : t + 1])
+
+        def il(gi, h, q, parts=2):
+            key = ("gi", gi, h)
+            if key not in st:
+                st[key] = ring.tile([P, 512, 4], BF16, name="xi", align_bytes=64, bufs=3)
+            w = 512 // parts
+            nc.scalar.copy(
+                out=st[key][:, w * q : w * q + w, :],
+                in_=xm[gi][:, :, 512 * h + w * q : 512 * h + w * q + w].rearrange("p t n -> p n t"),
+            )
+
+        def qg(gi, h):
+            sl = slice(512 * h, 512 * h + 512)
+            nc.vector.quantize_mx(
+                out=g_q[gi][:, sl].bitcast(FP8X4), scales=g_s[gi][:, sl],
+                in_=st["gi", gi, h][:].rearrange("p n t -> p (n t)"),
+            )
+
+        def ki(h, q, eng):
+            sl = slice(512 * h + 256 * q, 512 * h + 256 * q + 256)
+            src = k_sb[:, :, sl].rearrange("p t n -> p n t")
+            if eng == "g":
+                nc.gpsimd.tensor_scalar(out=k_i[:, sl, :], in0=src, scalar1=1.0, scalar2=0.0, op0=MULT, op1=ADD)
+            else:
+                nc.vector.tensor_copy(out=k_i[:, sl, :], in_=src)
+
+        def qk(h):
+            sl = slice(512 * h, 512 * h + 512)
+            nc.vector.quantize_mx(
+                out=k_q[:, sl].bitcast(FP8X4), scales=k_s[:, sl],
+                in_=k_i[:, sl, :].rearrange("p n t -> p (n t)"),
+            )
+
+        def m1(ti):
+            pi, j = divmod(ti, 2)
+            ps = psum_o.tile([P, 512], F32, name="acc")
+            for ng in range(2):
+                nc.tensor.matmul_mx(
+                    out=ps[:],
+                    lhsT=x_q[pi][:, ng, 128 * j : 128 * j + 128].bitcast(FP8X4),
+                    lhsT_scale=x_s[pi][:, ng, 128 * j : 128 * j + 128],
+                    rhs=c_q[:, ng, :].bitcast(FP8X4),
+                    rhs_scale=c_s[:, ng, :],
+                    start=(ng == 0), stop=(ng == 1),
+                )
+            st["z", ti] = ps
+
+        def nu(ti):
+            gi, t = divmod(ti, 4)
+            if ("nu", ti // 2) not in st:
+                st["nu", ti // 2] = ring.tile([P, 2, 512], BF16, name="nu", align_bytes=64, bufs=4)
+            nc.vector.tensor_tensor(
+                out=st["nu", ti // 2][:, ti % 2, :].rearrange("p (u w e) -> p u w e", u=2, e=2),
+                in0=y_sb[gi][:, t, :].rearrange("p (w u e) -> p u w e", u=2, e=2),
+                in1=st["z", ti][:].rearrange("p (w u e) -> p u w e", u=2, e=2),
+                op=SUB,
+            )
+
+        def tn(pi):
+            ps = psum_t.tile([P, 512], F32, name="tp")
+            for u in range(2):
+                for j in range(2):
+                    w = words(st["nu", pi][:, j, :])
+                    nc.tensor.transpose(
+                        ps[:, 256 * u + 128 * j : 256 * u + 128 * j + 128], w[:, 128 * u : 128 * u + 128], ident[:]
+                    )
+            st["tn", pi] = ps
+
+        def en(pi):
+            nt = ring.tile([P, 1024], BF16, name="nt", align_bytes=64, bufs=3)
+            nc.scalar.copy(
+                out=nt[:].bitcast(F32).rearrange("p (s u) -> p s u", u=2),
+                in_=st["tn", pi][:].rearrange("p (u s) -> p s u", u=2),
+            )
+            st["nt", pi] = nt
+
+        def qn(pi):
+            nc.vector.quantize_mx(out=n_q[pi][:].bitcast(FP8X4), scales=n_s[pi][:], in_=st["nt", pi][:])
+
+        def ta(ti):
+            gi, t = divmod(ti, 4)
+            ps = psum_t.tile([P, 512], F32, name="tp")
+            w = words(a_sb[gi][:, t, :])
+            for jg in range(2):
+                for u in range(2):
+                    nc.tensor.transpose(
+                        ps[:, 256 * jg + 128 * u : 256 * jg + 128 * u + 128],
+                        w[:, 256 * jg + u : 256 * (jg + 1) : 2],
+                        ident[:],
+                    )
+            st["ta", ti] = ps
+
+        def ea(ti):
+            at = ring.tile([P, 2, 128, 4], BF16, name="at", align_bytes=64, bufs=6)
+            nc.scalar.copy(
+                out=at[:].rearrange("p j i t -> p (j i t)").bitcast(F32).rearrange("p (j i u) -> p j i u", j=2, u=2),
+                in_=st["ta", ti][:].rearrange("p (j u i) -> p j i u", j=2, u=2),
+            )
+            st["at", ti] = at
+
+        def qa(ti):
+            nc.vector.quantize_mx(
+                out=a_q[ti][:].rearrange("p j i -> p (j i)").bitcast(FP8X4),
+                scales=a_s[ti][:].rearrange("p j i -> p (j i)"),
+                in_=st["at", ti][:].rearrange("p j i t -> p (j i t)"),
+            )
+
+        def deg(pi):
+            ps = psum_o.tile([P, 2], F32, name="acc")
+            for j in range(2):
+                at = st["at", 2 * pi + j]
+                for jg in range(2):
+                    for t in range(4):
+                        nc.tensor.matmul(
+                            ps[:, j : j + 1], at[:, jg, :, t], hg[:, jg, t : t + 1],
+                            start=(jg == 0 and t == 0), stop=(jg == 1 and t == 3),
+                        )
+            st["dg", pi] = ps
+
+        def ddo(pi):
+            nc.vector.tensor_scalar(
+                out=dd[:, 2 * pi : 2 * pi + 2], in0=st["dg", pi][:], scalar1=-1.0, scalar2=1.0, op0=MULT, op1=ADD
+            )
+
+        def m2(ti, h):
+            pi, j = divmod(ti, 2)
+            sl = slice(512 * h, 512 * h + 512)
+            ps = psum_o.tile([P, 512], F32, name="acc")
+            for jg in range(2):
+                nc.tensor.matmul_mx(
+                    out=ps[:],
+                    lhsT=a_q[ti][:, jg, :].bitcast(FP8X4), lhsT_scale=a_s[ti][:, jg, :],
+                    rhs=g_q[jg][:, sl].bitcast(FP8X4), rhs_scale=g_s[jg][:, sl],
+                    start=(jg == 0), stop=False,
+                )
+            nc.tensor.matmul_mx(
+                out=ps[:],
+                lhsT=n_q[pi][:, 128 * j : 128 * j + 128].bitcast(FP8X4), lhsT_scale=n_s[pi][:, 128 * j : 128 * j + 128],
+                rhs=k_q[:, sl].bitcast(FP8X4), rhs_scale=k_s[:, sl],
+                start=False, stop=True,
+            )
+            st["m2", ti, h] = ps
+
+        def stt(ti, h):
+            gi, t = divmod(ti, 4)
+            if ("o", ti // 2, h) not in st:
+                st["o", ti // 2, h] = ring.tile([P, 2, 512], F32, name="o", align_bytes=64, bufs=4)
+            o = st["o", ti // 2, h]
+            nc.vector.scalar_tensor_tensor(
+                out=o[:, ti % 2, :], in0=x_sb[gi][:, t, 512 * h : 512 * h + 512], scalar=dd[:, ti : ti + 1],
+                in1=st["m2", ti, h][:], op0=MULT, op1=ADD,
+            )
+
+        out_r = out_0.rearrange("(g p t) n -> g p t n", g=2, t=4)
+
+        def so(pi, h):
+            gi, hf = divmod(pi, 2)
+            nc.sync.dma_start(
+                out=out_r[gi, :, 2 * hf : 2 * hf + 2, 512 * h : 512 * h + 512], in_=st["o", pi, h][:]
+            )
+
+        def rd(ti, h):
+            if ("ob", ti // 2, h) not in st:
+                st["ob", ti // 2, h] = ring.tile([P, 2, 512], BF16, name="ob", align_bytes=64, bufs=4)
+            nc.scalar.copy(
+                out=st["ob", ti // 2, h][:, ti % 2, :].rearrange("p (u w e) -> p u w e", u=2, e=2),
+                in_=st["o", ti // 2, h][:, ti % 2, :].rearrange("p (w u e) -> p u w e", u=2, e=2),
+            )
+
+        def to(pi, h):
+            ps = psum_t.tile([P, 512], F32, name="tp")
+            for u in range(2):
+                for j in range(2):
+                    w = words(st["ob", pi, h][:, j, :])
+                    nc.tensor.transpose(
+                        ps[:, 256 * u + 128 * j : 256 * u + 128 * j + 128], w[:, 128 * u : 128 * u + 128], ident[:]
+                    )
+            st["to", pi, h] = ps
+
+        def eo(pi, h):
+            gi, hf = divmod(pi, 2)
+            dst = o_t[h][gi][:].rearrange("p i t -> p (i t)").bitcast(F32).rearrange("p (i t u) -> p i t u", t=4, u=2)
+            nc.scalar.copy(
+                out=dst[:, :, 2 * hf : 2 * hf + 2, :],
+                in_=st["to", pi, h][:].rearrange("p (u t i) -> p i t u", u=2, t=2),
+            )
+
+        def qo(gi, h):
+            nc.vector.quantize_mx(
+                out=o_q[h][gi][:].bitcast(FP8X4), scales=o_s[h][gi][:], in_=o_t[h][gi][:].rearrange("p i t -> p (i t)")
+            )
+            nc.sync.dma_start(
+                out=out_1[h, :, 512 * gi : 512 * gi + 512, :].rearrange("p m t -> p (m t)").bitcast(I32),
+                in_=o_q[h][gi][:].bitcast(I32),
+            )
+            for q in range(4):
+                nc.scalar.dma_start(
+                    out=out_2[h, 4 * q : 4 * q + 4, 512 * gi : 512 * gi + 512].bitcast(I32),
+                    in_=o_s[h][gi][32 * q : 32 * q + 4, :].bitcast(I32),
+                )
+
+        done_o = {}
+
+        def run(n):
+            d = [int(z) for z in n if z in "0123456789"]
+            f = n[:2]
+            if f == "tx":
+                tx(d[0], d[1])
+            elif f == "xp":
+                xp(d[0], d[1])
+            elif f == "qx":
+                qx(d[0])
+            elif f == "mu":
+                mu(d[0], d[1])
+            elif f == "tc":
+                tcc(d[0], d[1])
+            elif f == "ec":
+                ec(d[0], d[1])
+            elif f == "qc":
+                qc(d[0])
+            elif f == "il":
+                il(d[0], d[1], d[2])
+            elif f == "qg":
+                qg(d[0], d[1])
+            elif f == "ki":
+                ki(d[0], d[1], KENG[d[0]])
+            elif f == "qk":
+                qk(d[0])
+            elif f == "m1":
+                m1(d[1])
+            elif f == "nu":
+                nu(d[0])
+            elif f == "ta":
+                ta(d[0])
+            elif f == "ea":
+                ea(d[0])
+            elif f == "qa":
+                qa(d[0])
+            elif f == "tn":
+                tn(d[0])
+            elif f == "en":
+                en(d[0])
+            elif f == "qn":
+                qn(d[0])
+            elif f == "dg":
+                deg(d[0])
+            elif f == "dd":
+                ddo(d[0])
+            elif f == "m2":
+                m2(d[1], d[2])
+            elif f == "st":
+                stt(d[0], d[1])
+                key = (d[0] // 2, d[1])
+                if key in done_o:
+                    so(d[0] // 2, d[1])
+                done_o[key] = 1
+            elif f == "rd":
+                rd(d[0], d[1])
+            elif f == "to":
+                to(d[0], d[1])
+            elif f == "eo":
+                eo(d[0], d[1])
+            elif f == "qo":
+                qo(d[0], d[1])
+
+        with tc.manual_schedule():
+            for n in ORDER.split():
+                run(n)

@@ -17,8 +17,9 @@ ADD = mybir.AluOpType.add
 SUB = mybir.AluOpType.subtract
 
 P = 128
-KENG = "vg"
-ORDER = "tx01 mu01 mu00 tx00 xp01 tx11 xp00 tx10 xp11 tc00 qx0 tc01 ec00 xp10 tc10 ec01 mu03 mu02 tc11 ec10 qx1 tx21 ec11 qc0 tx20 il000 qc1 tx31 mu13 m1_1 mu10 il001 mu12 m1_0 mu11 nu1 m1_3 il100 nu0 m1_2 xp20 tn0 xp21 il101 ta1 ki00 ta0 ki01 ea1 qx2 ea0 tx30 ki10 en0 nu3 ta3 nu2 ta2 ea3 ki11 qg10 dg0 ea2 qk0 m1_4 il111 qg00 m1_5 xp30 tn1 ta4 xp31 en1 ta5 qn0 ea4 qa0 dd0 dg1 qx3 ea5 m2_00 qa1 il010 nu5 ta6 nu4 il011 qa2 m2_10 qn1 st00 m1_6 ea6 dd1 qa3 m1_7 st10 rd00 m2_20 nu6 il110 nu7 tn2 qa4 ta7 en2 st20 tn3 ea7 qa5 dg2 qn2 rd10 qa6 m2_30 dd2 qa7 en3 qg11 m2_40 rd20 st30 dg3 qn3 rd30 st40 m2_50 dd3 qg01 rd40 m2_60 st50 qk1 to00 rd50 to10 st60 eo00 m2_70 eo10 m2_01 st70 rd60 qo00 m2_11 rd70 st01 to20 st11 to30 rd01 m2_21 eo20 eo30 m2_31 st21 rd11 qo10 m2_41 rd21 st31 m2_51 st41 rd31 to01 rd41 st51 to11 eo01 m2_61 eo11 m2_71 rd51 st61 qo01 to21 rd61 st71 eo21 rd71 to31 eo31 qo11"
+KENG = "gg"
+RENG = "SSSSSSSSSSSSSSSS"
+ORDER = "mu00 mu01 tx01 xp01 mu02 tx00 mu03 il001 tx10 xp10 tx11 xp11 xp00 qx1 qx0 mu11 tc01 ec01 tc11 ec11 tc00 mu10 ec00 tc10 qc1 tx20 mu13 tx21 ec10 qc0 ki01 il000 mu12 il100 tx31 xp21 xp20 tx30 xp30 xp31 m1_2 nu2 m1_1 m1_3 il101 il010 m1_0 ta1 qx2 qx3 ta2 ea2 nu3 ta3 ea3 il011 m1_4 tn1 en1 qg10 ta4 ea4 ta5 ea5 nu1 m1_7 qg00 ea1 nu4 m1_6 ta7 ea7 ki00 ta6 dg1 ea6 qa1 nu7 m1_5 ta0 nu0 nu6 tn0 qn1 tn3 dd1 nu5 qk0 ki11 en3 il110 dg3 ki10 qg01 dd3 qn3 qa3 m2_30 st30 m2_20 st20 qk1 il111 qg11 rd30 tn2 ea0 dg2 m2_60 m2_70 dd2 st60 en2 m2_31 rd20 st70 st31 qa2 rd70 rd31 qn2 m2_61 en0 st61 m2_21 st21 m2_71 st71 m2_50 m2_51 st50 qn0 rd61 rd60 to10 rd21 eo10 to30 rd50 to11 st51 eo11 qa0 dg0 rd71 rd51 dd0 m2_40 st40 m2_00 st00 eo30 m2_01 st01 rd40 rd00 rd01 m2_11 st11 m2_41 rd11 m2_10 to20 st41 rd41 st10 eo20 rd10 qo10 to01 eo01 to21 to31 eo31 to00 qo01 eo00 qo00 eo21 qo11"
 
 
 def tile_signedkalmanconsensusfilterstep_x1_kernel(tc, x, y, p, c, k, a, g, out_0, out_1, out_2):
@@ -40,12 +41,11 @@ def tile_signedkalmanconsensusfilterstep_x1_kernel(tc, x, y, p, c, k, a, g, out_
         x_sb = [kt("x_sb%d" % i, [P, 4, N], BF16) for i in range(2)]
         a_sb = [kt("a_sb%d" % i, [P, 4, S], BF16) for i in range(2)]
         y_sb = [kt("y_sb%d" % i, [P, 4, M], BF16) for i in range(2)]
-        c_sb = kt("c_sb", [P, 4, N], BF16)
-        k_sb = kt("k_sb", [P, 4, N], BF16)
-        c_t = kt("c_t", [P, 2, M, 4], BF16)
+        c_sb = keep.tile([P, 4, N], BF16, name="c_sb", tag="w0", align_bytes=64)
+        k_sb = keep.tile([P, 4, N], BF16, name="k_sb", tag="w1", align_bytes=64)
+        c_t = keep.tile([P, 2, M, 4], BF16, name="c_t", tag="w2", align_bytes=64)
         c_q = kt("c_q", [P, 2, M], U32)
         c_s = kt("c_s", [P, 2, M], U8)
-        k_i = kt("k_i", [P, N, 4], BF16)
         k_q = kt("k_q", [P, N], U32)
         k_s = kt("k_s", [P, N], U8)
         xm = [kt("xm%d" % i, [P, 4, N], BF16) for i in range(2)]
@@ -55,11 +55,10 @@ def tile_signedkalmanconsensusfilterstep_x1_kernel(tc, x, y, p, c, k, a, g, out_
         x_s = [kt("x_s%d" % i, [P, 2, 256], U8) for i in range(4)]
         n_q = [kt("n_q%d" % i, [P, 256], U32) for i in range(4)]
         n_s = [kt("n_s%d" % i, [P, 256], U8) for i in range(4)]
-        a_q = [kt("a_q%d" % i, [P, 2, P], U32) for i in range(8)]
-        a_s = [kt("a_s%d" % i, [P, 2, P], U8) for i in range(8)]
+        a_q = [kt("a_q%d" % i, [P, 2, 2, P], U32) for i in range(4)]
+        a_s = [kt("a_s%d" % i, [P, 2, 2, P], U8) for i in range(4)]
         o_q = [[kt("o_q%d%d" % (i, j), [P, M], U32) for j in range(2)] for i in range(2)]
         o_s = [[kt("o_s%d%d" % (i, j), [P, M], U8) for j in range(2)] for i in range(2)]
-        o_t = [[kt("o_t%d%d" % (i, 0), [P, 512, 4], BF16) for i in range(2)]] * 2
 
         nc.scalar.dma_start(out=p_t[:], in_=p.rearrange("(h q t) -> q h t", h=2, t=4))
         nc.scalar.dma_start(out=g_t[:], in_=g.rearrange("(h q t) -> q h t", h=2, t=4))
@@ -73,7 +72,8 @@ def tile_signedkalmanconsensusfilterstep_x1_kernel(tc, x, y, p, c, k, a, g, out_
         def ld(dst, src, i, hf):
             nc.sync.dma_start(out=dst[i][:, 2 * hf : 2 * hf + 2, :], in_=src[i, :, 2 * hf : 2 * hf + 2, :])
 
-        ld(x_sb, xr, 0, 0)
+        for t in range(2):
+            nc.sync.dma_start(out=x_sb[0][:, t, :], in_=xr[0, :, t, :])
         ld(x_sb, xr, 0, 1)
         for b in range(2):
             nc.sync.dma_start(out=c_sb[:, 2 * b : 2 * b + 2, :], in_=cr[:, 2 * b : 2 * b + 2, :])
@@ -110,7 +110,7 @@ def tile_signedkalmanconsensusfilterstep_x1_kernel(tc, x, y, p, c, k, a, g, out_
 
         def xp(pi, ng):
             if ("xt", pi) not in st:
-                xt = ring.tile([P, 2, 1024], BF16, name="xt", align_bytes=64, bufs=3)
+                xt = ring.tile([P, 2, 1024], BF16, name="xt", align_bytes=64, bufs=4)
                 st["xt", pi] = xt
             xt = st["xt", pi]
             if True:
@@ -160,7 +160,7 @@ def tile_signedkalmanconsensusfilterstep_x1_kernel(tc, x, y, p, c, k, a, g, out_
         def il(gi, h, q, parts=2):
             key = ("gi", gi, h)
             if key not in st:
-                st[key] = ring.tile([P, 512, 4], BF16, name="xi", align_bytes=64, bufs=3)
+                st[key] = ring.tile([P, 512, 4], BF16, name="xi", align_bytes=64, bufs=4)
             w = 512 // parts
             nc.scalar.copy(
                 out=st[key][:, w * q : w * q + w, :],
@@ -175,6 +175,9 @@ def tile_signedkalmanconsensusfilterstep_x1_kernel(tc, x, y, p, c, k, a, g, out_
             )
 
         def ki(h, q, eng):
+            if "k_i" not in st:
+                st["k_i"] = keep.tile([P, N, 4], BF16, name="k_i", tag="w2", align_bytes=64)
+            k_i = st["k_i"]
             sl = slice(512 * h + 256 * q, 512 * h + 256 * q + 256)
             src = k_sb[:, :, sl].rearrange("p t n -> p n t")
             if eng == "g":
@@ -186,7 +189,7 @@ def tile_signedkalmanconsensusfilterstep_x1_kernel(tc, x, y, p, c, k, a, g, out_
             sl = slice(512 * h, 512 * h + 512)
             nc.vector.quantize_mx(
                 out=k_q[:, sl].bitcast(FP8X4), scales=k_s[:, sl],
-                in_=k_i[:, sl, :].rearrange("p n t -> p (n t)"),
+                in_=st["k_i"][:, sl, :].rearrange("p n t -> p (n t)"),
             )
 
         def m1(ti):
@@ -225,7 +228,7 @@ def tile_signedkalmanconsensusfilterstep_x1_kernel(tc, x, y, p, c, k, a, g, out_
             st["tn", pi] = ps
 
         def en(pi):
-            nt = ring.tile([P, 1024], BF16, name="nt", align_bytes=64, bufs=3)
+            nt = ring.tile([P, 1024], BF16, name="nt", align_bytes=64, bufs=4)
             nc.scalar.copy(
                 out=nt[:].bitcast(F32).rearrange("p (s u) -> p s u", u=2),
                 in_=st["tn", pi][:].rearrange("p (u s) -> p s u", u=2),
@@ -249,24 +252,26 @@ def tile_signedkalmanconsensusfilterstep_x1_kernel(tc, x, y, p, c, k, a, g, out_
             st["ta", ti] = ps
 
         def ea(ti):
-            at = ring.tile([P, 2, 128, 4], BF16, name="at", align_bytes=64, bufs=6)
+            pi, j = divmod(ti, 2)
+            if ("at", pi) not in st:
+                st["at", pi] = ring.tile([P, 2, 2, 128, 4], BF16, name="at", align_bytes=64, bufs=4)
+            at = st["at", pi]
             nc.scalar.copy(
-                out=at[:].rearrange("p j i t -> p (j i t)").bitcast(F32).rearrange("p (j i u) -> p j i u", j=2, u=2),
+                out=at[:, j].rearrange("p j i t -> p (j i t)").bitcast(F32).rearrange("p (j i u) -> p j i u", j=2, u=2),
                 in_=st["ta", ti][:].rearrange("p (j u i) -> p j i u", j=2, u=2),
             )
-            st["at", ti] = at
 
-        def qa(ti):
+        def qa(pi):
             nc.vector.quantize_mx(
-                out=a_q[ti][:].rearrange("p j i -> p (j i)").bitcast(FP8X4),
-                scales=a_s[ti][:].rearrange("p j i -> p (j i)"),
-                in_=st["at", ti][:].rearrange("p j i t -> p (j i t)"),
+                out=a_q[pi][:].rearrange("p b j i -> p (b j i)").bitcast(FP8X4),
+                scales=a_s[pi][:].rearrange("p b j i -> p (b j i)"),
+                in_=st["at", pi][:].rearrange("p b j i t -> p (b j i t)"),
             )
 
         def deg(pi):
             ps = psum_o.tile([P, 2], F32, name="acc")
             for j in range(2):
-                at = st["at", 2 * pi + j]
+                at = st["at", pi][:, j]
                 for jg in range(2):
                     for t in range(4):
                         nc.tensor.matmul(
@@ -287,7 +292,7 @@ def tile_signedkalmanconsensusfilterstep_x1_kernel(tc, x, y, p, c, k, a, g, out_
             for jg in range(2):
                 nc.tensor.matmul_mx(
                     out=ps[:],
-                    lhsT=a_q[ti][:, jg, :].bitcast(FP8X4), lhsT_scale=a_s[ti][:, jg, :],
+                    lhsT=a_q[pi][:, j, jg, :].bitcast(FP8X4), lhsT_scale=a_s[pi][:, j, jg, :],
                     rhs=g_q[jg][:, sl].bitcast(FP8X4), rhs_scale=g_s[jg][:, sl],
                     start=(jg == 0), stop=False,
                 )
@@ -301,29 +306,31 @@ def tile_signedkalmanconsensusfilterstep_x1_kernel(tc, x, y, p, c, k, a, g, out_
 
         def stt(ti, h):
             gi, t = divmod(ti, 4)
-            if ("o", ti // 2, h) not in st:
-                st["o", ti // 2, h] = ring.tile([P, 2, 512], F32, name="o", align_bytes=64, bufs=4)
-            o = st["o", ti // 2, h]
+            o = ring.tile([P, 512], F32, name="o", align_bytes=64, bufs=8)
+            st["o", ti, h] = o
             nc.vector.scalar_tensor_tensor(
-                out=o[:, ti % 2, :], in0=x_sb[gi][:, t, 512 * h : 512 * h + 512], scalar=dd[:, ti : ti + 1],
+                out=o[:], in0=x_sb[gi][:, t, 512 * h : 512 * h + 512], scalar=dd[:, ti : ti + 1],
                 in1=st["m2", ti, h][:], op0=MULT, op1=ADD,
             )
 
         out_r = out_0.rearrange("(g p t) n -> g p t n", g=2, t=4)
 
-        def so(pi, h):
-            gi, hf = divmod(pi, 2)
-            nc.sync.dma_start(
-                out=out_r[gi, :, 2 * hf : 2 * hf + 2, 512 * h : 512 * h + 512], in_=st["o", pi, h][:]
-            )
+        def so(ti, h):
+            gi, t = divmod(ti, 4)
+            nc.sync.dma_start(out=out_r[gi, :, t, 512 * h : 512 * h + 512], in_=st["o", ti, h][:])
 
         def rd(ti, h):
             if ("ob", ti // 2, h) not in st:
-                st["ob", ti // 2, h] = ring.tile([P, 2, 512], BF16, name="ob", align_bytes=64, bufs=4)
-            nc.scalar.copy(
-                out=st["ob", ti // 2, h][:, ti % 2, :].rearrange("p (u w e) -> p u w e", u=2, e=2),
-                in_=st["o", ti // 2, h][:, ti % 2, :].rearrange("p (w u e) -> p u w e", u=2, e=2),
-            )
+                st["ob", ti // 2, h] = ring.tile([P, 2, 512], BF16, name="ob", align_bytes=64, bufs=5)
+            dst = st["ob", ti // 2, h][:, ti % 2, :].rearrange("p (u w e) -> p u w e", u=2, e=2)
+            src = st["o", ti, h][:].rearrange("p (w u e) -> p u w e", u=2, e=2)
+            e = RENG[ti + 8 * h]
+            if e == "G":
+                nc.gpsimd.tensor_scalar(out=dst, in0=src, scalar1=1.0, scalar2=0.0, op0=MULT, op1=ADD)
+            elif e == "V":
+                nc.vector.tensor_copy(out=dst, in_=src)
+            else:
+                nc.scalar.copy(out=dst, in_=src)
 
         def to(pi, h):
             ps = psum_t.tile([P, 512], F32, name="tp")
@@ -337,7 +344,9 @@ def tile_signedkalmanconsensusfilterstep_x1_kernel(tc, x, y, p, c, k, a, g, out_
 
         def eo(pi, h):
             gi, hf = divmod(pi, 2)
-            dst = o_t[h][gi][:].rearrange("p i t -> p (i t)").bitcast(F32).rearrange("p (i t u) -> p i t u", t=4, u=2)
+            if ("o_t", h) not in st:
+                st["o_t", h] = keep.tile([P, 2, 512, 4], BF16, name="o_t%d" % h, tag="w%d" % h, align_bytes=64)
+            dst = st["o_t", h][:, gi].rearrange("p i t -> p (i t)").bitcast(F32).rearrange("p (i t u) -> p i t u", t=4, u=2)
             nc.scalar.copy(
                 out=dst[:, :, 2 * hf : 2 * hf + 2, :],
                 in_=st["to", pi, h][:].rearrange("p (u t i) -> p i t u", u=2, t=2),
@@ -345,7 +354,7 @@ def tile_signedkalmanconsensusfilterstep_x1_kernel(tc, x, y, p, c, k, a, g, out_
 
         def qo(gi, h):
             nc.vector.quantize_mx(
-                out=o_q[h][gi][:].bitcast(FP8X4), scales=o_s[h][gi][:], in_=o_t[h][gi][:].rearrange("p i t -> p (i t)")
+                out=o_q[h][gi][:].bitcast(FP8X4), scales=o_s[h][gi][:], in_=st["o_t", h][:, gi].rearrange("p i t -> p (i t)")
             )
             nc.sync.dma_start(
                 out=out_1[h, :, 512 * gi : 512 * gi + 512, :].rearrange("p m t -> p (m t)").bitcast(I32),
@@ -357,7 +366,6 @@ def tile_signedkalmanconsensusfilterstep_x1_kernel(tc, x, y, p, c, k, a, g, out_
                     in_=o_s[h][gi][32 * q : 32 * q + 4, :].bitcast(I32),
                 )
 
-        done_o = {}
 
         def run(n):
             d = [int(z) for z in n if z in "0123456789"]
@@ -408,10 +416,7 @@ def tile_signedkalmanconsensusfilterstep_x1_kernel(tc, x, y, p, c, k, a, g, out_
                 m2(d[1], d[2])
             elif f == "st":
                 stt(d[0], d[1])
-                key = (d[0] // 2, d[1])
-                if key in done_o:
-                    so(d[0] // 2, d[1])
-                done_o[key] = 1
+                so(d[0], d[1])
             elif f == "rd":
                 rd(d[0], d[1])
             elif f == "to":

@@ -15,414 +15,344 @@ FP8X4 = mybir.dt.float8_e4m3fn_x4
 MULT = mybir.AluOpType.mult
 ADD = mybir.AluOpType.add
 SUB = mybir.AluOpType.subtract
+COPY = mybir.ActivationFunctionType.Copy
 
 P = 128
-KENG = "gg"
-RENG = "SSSSSSSSSSSSSSSS"
-ORDER = "mu00 mu01 tx01 xp01 mu02 tx00 mu03 il001 tx10 xp10 tx11 xp11 xp00 qx1 qx0 mu11 tc01 ec01 tc11 ec11 tc00 mu10 ec00 tc10 qc1 tx20 mu13 tx21 ec10 qc0 ki01 il000 mu12 il100 tx31 xp21 xp20 tx30 xp30 xp31 m1_2 nu2 m1_1 m1_3 il101 il010 m1_0 ta1 qx2 qx3 ta2 ea2 nu3 ta3 ea3 il011 m1_4 tn1 en1 qg10 ta4 ea4 ta5 ea5 nu1 m1_7 qg00 ea1 nu4 m1_6 ta7 ea7 ki00 ta6 dg1 ea6 qa1 nu7 m1_5 ta0 nu0 nu6 tn0 qn1 tn3 dd1 nu5 qk0 ki11 en3 il110 dg3 ki10 qg01 dd3 qn3 qa3 m2_30 st30 m2_20 st20 qk1 il111 qg11 rd30 tn2 ea0 dg2 m2_60 m2_70 dd2 st60 en2 m2_31 rd20 st70 st31 qa2 rd70 rd31 qn2 m2_61 en0 st61 m2_21 st21 m2_71 st71 m2_50 m2_51 st50 qn0 rd61 rd60 to10 rd21 eo10 to30 rd50 to11 st51 eo11 qa0 dg0 rd71 rd51 dd0 m2_40 st40 m2_00 st00 eo30 m2_01 st01 rd40 rd00 rd01 m2_11 st11 m2_41 rd11 m2_10 to20 st41 rd41 st10 eo20 rd10 qo10 to01 eo01 to21 to31 eo31 to00 qo01 eo00 qo00 eo21 qo11"
+MENG = "SSSVVVVV"
+QA, QN, DQ, RP = 4, 2, 4, 1
+ORDER = "tx00 mu00 tx01 xp00 mu01 xp01 mu02 tx10 tx11 xp10 xp11 tc00 tc01 ec00 tc10 ec01 ki00 qx0 mu03 ki01 mu10 ec10 qx1 mu11 tc11 tx20 ec11 tx21 qc0 il00 tx30 mu12 mu13 tx31 m1_0 xp20 il10 xp21 m1_1 m1_2 xp30 ta0 qx2 ta1 ta2 nu0 m1_3 ki02 nu1 xp31 ki03 m1_4 ki10 nu2 ea0 ta3 ea1 tn0 nu3 ta4 ea2 m1_5 tn1 ea3 qx3 qk0 ta5 en0 qa0 ki11 ea4 ta6 nu4 en1 m1_6 ea5 dg0 qg0 nu5 m1_7 ta7 dd0 ki12 qn0 nu6 il01 nu7 ea6 tn2 en2 ea7 m2_00 m2_10 ki13 tn3 dg1 st00 en3 m2_20 m2_30 qk1 il11 qa1 qn1 dd1 st10 st20 st30 m2_40 st40 rd00 m2_50 qg1 rd10 st50 m2_60 to00 m2_70 st60 eo00 st70 m2_01 st01 rd20 m2_11 m2_21 m2_31 st11 rd30 to10 rd01 st21 to20 to30 st31 eo10 eo20 m2_41 qo00 eo30 m2_51 st41 m2_61 rd11 st51 m2_71 st61 to01 to11 rd21 st71 rv6 rv7 eo01 to21 eo11 to31 qo10 eo21 qo01 eo31 fo31 qp11 qo11"
 
 
 def tile_signedkalmanconsensusfilterstep_x1_kernel(tc, x, y, p, c, k, a, g, out_0, out_1, out_2):
     nc = tc.nc
     with ExitStack() as ctx:
         keep = ctx.enter_context(tc.tile_pool(name="keep", bufs=1))
-        ring = ctx.enter_context(tc.tile_pool(name="ring", bufs=2))
+        ring = ctx.enter_context(tc.tile_pool(name="ring", bufs=4))
         psum_t = ctx.enter_context(tc.psum_pool(name="psum_t", bufs=4))
         psum_o = ctx.enter_context(tc.psum_pool(name="psum_o", bufs=4))
 
-        def kt(name, shape, dtype):
-            return keep.tile(shape, dtype, name=name, align_bytes=64)
+        def kt(name, shape, dtype, tag=None):
+            return keep.tile(shape, dtype, name=name, tag=tag or name, align_bytes=64)
+
+        def rt(name, shape, dtype, bufs):
+            return ring.tile(shape, dtype, name=name, align_bytes=64, bufs=bufs)
 
         ident = kt("ident", [P, P], F32)
         p_t = kt("p_t", [P, 2, 4], BF16)
         g_t = kt("g_t", [P, 2, 4], BF16)
         hg = kt("hg", [P, 2, 4], BF16)
+        hgf = kt("hgf", [P, 2, 4], F32)
         dd = kt("dd", [P, 8], F32)
         x_sb = [kt("x_sb%d" % i, [P, 4, N], BF16) for i in range(2)]
         a_sb = [kt("a_sb%d" % i, [P, 4, S], BF16) for i in range(2)]
         y_sb = [kt("y_sb%d" % i, [P, 4, M], BF16) for i in range(2)]
-        c_sb = keep.tile([P, 4, N], BF16, name="c_sb", tag="w0", align_bytes=64)
-        k_sb = keep.tile([P, 4, N], BF16, name="k_sb", tag="w1", align_bytes=64)
-        c_t = keep.tile([P, 2, M, 4], BF16, name="c_t", tag="w2", align_bytes=64)
+        c_sb = kt("c_sb", [P, 4, N], BF16, "w0")
+        k_sb = kt("k_sb", [P, 4, N], BF16, "w1")
+        c_t = kt("c_t", [P, 2, M, 4], BF16, "w2")
         c_q = kt("c_q", [P, 2, M], U32)
         c_s = kt("c_s", [P, 2, M], U8)
         k_q = kt("k_q", [P, N], U32)
         k_s = kt("k_s", [P, N], U8)
         xm = [kt("xm%d" % i, [P, 4, N], BF16) for i in range(2)]
-        g_q = [kt("g_q%d" % i, [P, N], U32) for i in range(2)]
-        g_s = [kt("g_s%d" % i, [P, N], U8) for i in range(2)]
+        g_q = [kt("g_q%d" % i, [P, 2, 512], U32) for i in range(2)]
+        g_s = [kt("g_s%d" % i, [P, 2, 512], U8) for i in range(2)]
         x_q = [kt("x_q%d" % i, [P, 2, 256], U32) for i in range(4)]
         x_s = [kt("x_s%d" % i, [P, 2, 256], U8) for i in range(4)]
-        n_q = [kt("n_q%d" % i, [P, 256], U32) for i in range(4)]
-        n_s = [kt("n_s%d" % i, [P, 256], U8) for i in range(4)]
-        a_q = [kt("a_q%d" % i, [P, 2, 2, P], U32) for i in range(4)]
-        a_s = [kt("a_s%d" % i, [P, 2, 2, P], U8) for i in range(4)]
-        o_q = [[kt("o_q%d%d" % (i, j), [P, M], U32) for j in range(2)] for i in range(2)]
-        o_s = [[kt("o_s%d%d" % (i, j), [P, M], U8) for j in range(2)] for i in range(2)]
+        n_q = kt("n_q", [P, S], U32)
+        n_s = kt("n_s", [P, S], U8)
+        a_q = kt("a_q", [P, 8, 2, P], U32)
+        a_s = kt("a_s", [P, 8, 2, P], U8)
+        o_q = [[kt("o_q%d%d" % (i, j), [P, 512], U32) for j in range(2)] for i in range(2)]
+        o_s = [[kt("o_s%d%d" % (i, j), [P, 512], U8) for j in range(2)] for i in range(2)]
+        nt = kt("nt", [P, S, 4], BF16)
+        at = kt("at", [P, 8, 2, P, 4], BF16)
 
-        nc.scalar.dma_start(out=p_t[:], in_=p.rearrange("(h q t) -> q h t", h=2, t=4))
         nc.scalar.dma_start(out=g_t[:], in_=g.rearrange("(h q t) -> q h t", h=2, t=4))
+        nc.scalar.dma_start(out=p_t[:], in_=p.rearrange("(h q t) -> q h t", h=2, t=4))
         make_identity(nc, ident[:])
         xr = x.rearrange("(g p t) n -> g p t n", g=2, t=4)
         ar = a.rearrange("(g p t) n -> g p t n", g=2, t=4)
         yr = y.rearrange("(g p t) n -> g p t n", g=2, t=4)
         cr = c.rearrange("(b p) n -> p b n", p=P)
         kr = k.rearrange("(p t) n -> p t n", t=4)
-
-        def ld(dst, src, i, hf):
-            nc.sync.dma_start(out=dst[i][:, 2 * hf : 2 * hf + 2, :], in_=src[i, :, 2 * hf : 2 * hf + 2, :])
-
+        lo, hi = slice(0, 2), slice(2, 4)
         for t in range(2):
             nc.sync.dma_start(out=x_sb[0][:, t, :], in_=xr[0, :, t, :])
-        ld(x_sb, xr, 0, 1)
-        for b in range(2):
-            nc.sync.dma_start(out=c_sb[:, 2 * b : 2 * b + 2, :], in_=cr[:, 2 * b : 2 * b + 2, :])
-        ld(x_sb, xr, 1, 0)
-        ld(x_sb, xr, 1, 1)
+        nc.sync.dma_start(out=x_sb[0][:, hi, :], in_=xr[0, :, hi, :])
+        nc.sync.dma_start(out=c_sb[:, lo, :], in_=cr[:, lo, :])
+        nc.sync.dma_start(out=c_sb[:, hi, :], in_=cr[:, hi, :])
+        nc.sync.dma_start(out=x_sb[1][:, lo, :], in_=xr[1, :, lo, :])
+        nc.sync.dma_start(out=x_sb[1][:, hi, :], in_=xr[1, :, hi, :])
         nc.sync.dma_start(out=y_sb[0][:], in_=yr[0])
         nc.sync.dma_start(out=k_sb[:, :, 0:512], in_=kr[:, :, 0:512])
-        ld(a_sb, ar, 0, 0)
-        ld(a_sb, ar, 0, 1)
+        nc.sync.dma_start(out=a_sb[0][:, lo, :], in_=ar[0, :, lo, :])
+        nc.sync.dma_start(out=a_sb[0][:, hi, :], in_=ar[0, :, hi, :])
         nc.sync.dma_start(out=k_sb[:, :, 512:1024], in_=kr[:, :, 512:1024])
-        ld(a_sb, ar, 1, 0)
+        nc.sync.dma_start(out=a_sb[1][:, lo, :], in_=ar[1, :, lo, :])
         nc.sync.dma_start(out=y_sb[1][:], in_=yr[1])
-        ld(a_sb, ar, 1, 1)
+        nc.sync.dma_start(out=a_sb[1][:, hi, :], in_=ar[1, :, hi, :])
+        nc.vector.tensor_scalar_mul(hgf[:], g_t[:], 0.5)
         nc.vector.tensor_scalar_mul(hg[:], g_t[:], 0.5)
 
         st = {}
 
-        def words(t2d):
-            return t2d.bitcast(F32)
+        def turn(rows, col):
+            ps = psum_t.tile([P, 512], F32, name="tp")
+            for u in range(2):
+                for j in range(2):
+                    nc.tensor.transpose(
+                        ps[:, 256 * u + 128 * j : 256 * u + 128 * j + 128], rows[j].bitcast(F32)[:, col(u)], ident[:]
+                    )
+            return ps
+
+        def every2(ng):
+            return lambda u: slice(256 * ng + u, 256 * ng + 256, 2)
+
+        def turn_packed(src):
+            ps = psum_t.tile([P, 512], F32, name="tp")
+            for o in range(0, 512, 128):
+                nc.tensor.transpose(ps[:, o : o + 128], src.bitcast(F32)[:, o : o + 128], ident[:])
+            return ps
+
+        def wout(ap):
+            return ap.bitcast(F32).rearrange("p (r u) -> p r u", u=2)
+
+        def win(ps):
+            return ps[:].rearrange("p (u r) -> p r u", u=2)
+
+        def quant(q, s, src):
+            nc.vector.quantize_mx(out=q.bitcast(FP8X4), scales=s, in_=src)
+
+        def mx(ps, lq, ls, rq, rs, first, last):
+            nc.tensor.matmul_mx(
+                out=ps[:], lhsT=lq.bitcast(FP8X4), lhsT_scale=ls, rhs=rq.bitcast(FP8X4), rhs_scale=rs, start=first, stop=last
+            )
 
         def tx(pi, ng):
             gi, hf = divmod(pi, 2)
-            if True:
-                ps = psum_t.tile([P, 512], F32, name="tp")
-                for u in range(2):
-                    for j in range(2):
-                        w = words(x_sb[gi][:, 2 * hf + j, :])
-                        nc.tensor.transpose(
-                            ps[:, 256 * u + 128 * j : 256 * u + 128 * j + 128],
-                            w[:, 256 * ng + u : 256 * (ng + 1) : 2],
-                            ident[:],
-                        )
-                st["tx", pi, ng] = ps
+            st["tx", pi, ng] = turn([x_sb[gi][:, 2 * hf + j, :] for j in range(2)], every2(ng))
 
         def xp(pi, ng):
-            if ("xt", pi) not in st:
-                xt = ring.tile([P, 2, 1024], BF16, name="xt", align_bytes=64, bufs=4)
-                st["xt", pi] = xt
-            xt = st["xt", pi]
-            if True:
-                ps = st["tx", pi, ng]
-                nc.vector.tensor_tensor(
-                    out=xt[:, ng, :].rearrange("p (s u e) -> p s u e", u=2, e=2),
-                    in0=ps[:].bitcast(BF16).rearrange("p (u s e) -> p s u e", u=2, e=2),
-                    in1=p_t[:, ng, :].rearrange("p (u e) -> p u e", e=2).unsqueeze(1).broadcast_to([P, 256, 2, 2]),
-                    op=MULT,
-                )
+            if ng == 0:
+                st["xt", pi] = rt("xt", [P, 2, 1024], BF16, 3)
+            nc.vector.tensor_tensor(
+                out=st["xt", pi][:, ng, :].rearrange("p (s u e) -> p s u e", u=2, e=2),
+                in0=st["tx", pi, ng][:].bitcast(BF16).rearrange("p (u s e) -> p s u e", u=2, e=2),
+                in1=p_t[:, ng, :].rearrange("p (u e) -> p u e", e=2).unsqueeze(1).broadcast_to([P, 256, 2, 2]),
+                op=MULT,
+            )
 
         def qx(pi):
-            nc.vector.quantize_mx(
-                out=x_q[pi][:].rearrange("p a b -> p (a b)").bitcast(FP8X4),
-                scales=x_s[pi][:].rearrange("p a b -> p (a b)"),
-                in_=st["xt", pi][:].rearrange("p a b -> p (a b)"),
+            quant(
+                x_q[pi][:].rearrange("p n s -> p (n s)"), x_s[pi][:].rearrange("p n s -> p (n s)"),
+                st["xt", pi][:].rearrange("p n s -> p (n s)"),
             )
 
         def tcc(b, ng):
-            if True:
-                ps = psum_t.tile([P, 512], F32, name="tp")
-                for u in range(2):
-                    for j in range(2):
-                        w = words(c_sb[:, 2 * b + j, :])
-                        nc.tensor.transpose(
-                            ps[:, 256 * u + 128 * j : 256 * u + 128 * j + 128],
-                            w[:, 256 * ng + u : 256 * (ng + 1) : 2],
-                            ident[:],
-                        )
-                st["tc", b, ng] = ps
+            st["tc", b, ng] = turn([c_sb[:, 2 * b + j, :] for j in range(2)], every2(ng))
 
         def ec(b, ng):
             nc.scalar.copy(
-                out=c_t[:, ng, 256 * b : 256 * b + 256, :].rearrange("p m t -> p (m t)").bitcast(F32).rearrange("p (m u) -> p m u", u=2),
-                in_=st["tc", b, ng][:].rearrange("p (u m) -> p m u", u=2),
+                out=wout(c_t[:, ng, 256 * b : 256 * b + 256, :].rearrange("p m t -> p (m t)")), in_=win(st["tc", b, ng])
             )
 
-        def qc(ng):
-            nc.vector.quantize_mx(
-                out=c_q[:, ng, :].bitcast(FP8X4), scales=c_s[:, ng, :],
-                in_=c_t[:, ng, :, :].rearrange("p m t -> p (m t)"),
-            )
+        def qc():
+            quant(c_q[:].rearrange("p n m -> p (n m)"), c_s[:].rearrange("p n m -> p (n m)"), c_t[:].rearrange("p n m t -> p (n m t)"))
 
         def mu(gi, t):
-            nc.vector.tensor_scalar_mul(xm[gi][:, t, :], x_sb[gi][:, t, :], hg[:, gi, t : t + 1])
-
-        def il(gi, h, q, parts=2):
-            key = ("gi", gi, h)
-            if key not in st:
-                st[key] = ring.tile([P, 512, 4], BF16, name="xi", align_bytes=64, bufs=4)
-            w = 512 // parts
-            nc.scalar.copy(
-                out=st[key][:, w * q : w * q + w, :],
-                in_=xm[gi][:, :, 512 * h + w * q : 512 * h + w * q + w].rearrange("p t n -> p n t"),
-            )
-
-        def qg(gi, h):
-            sl = slice(512 * h, 512 * h + 512)
-            nc.vector.quantize_mx(
-                out=g_q[gi][:, sl].bitcast(FP8X4), scales=g_s[gi][:, sl],
-                in_=st["gi", gi, h][:].rearrange("p n t -> p (n t)"),
-            )
-
-        def ki(h, q, eng):
-            if "k_i" not in st:
-                st["k_i"] = keep.tile([P, N, 4], BF16, name="k_i", tag="w2", align_bytes=64)
-            k_i = st["k_i"]
-            sl = slice(512 * h + 256 * q, 512 * h + 256 * q + 256)
-            src = k_sb[:, :, sl].rearrange("p t n -> p n t")
-            if eng == "g":
-                nc.gpsimd.tensor_scalar(out=k_i[:, sl, :], in0=src, scalar1=1.0, scalar2=0.0, op0=MULT, op1=ADD)
+            if MENG[4 * gi + t] == "S":
+                nc.scalar.activation(out=xm[gi][:, t, :], in_=x_sb[gi][:, t, :], func=COPY, scale=hgf[:, gi, t : t + 1])
             else:
-                nc.vector.tensor_copy(out=k_i[:, sl, :], in_=src)
+                nc.vector.tensor_scalar_mul(xm[gi][:, t, :], x_sb[gi][:, t, :], hgf[:, gi, t : t + 1])
+
+        def il(gi, h):
+            if gi == 0:
+                st["xi", h] = rt("xi", [P, 2, 512, 4], BF16, 2)
+            nc.scalar.copy(
+                out=st["xi", h][:, gi], in_=xm[gi][:, :, 512 * h : 512 * h + 512].rearrange("p t n -> p n t")
+            )
+
+        def qg(h):
+            quant(
+                g_q[h][:].rearrange("p g n -> p (g n)"), g_s[h][:].rearrange("p g n -> p (g n)"),
+                st["xi", h][:].rearrange("p g n t -> p (g n t)"),
+            )
+
+        def ki(h, q):
+            if (h, q) == (0, 0):
+                st["k_i"] = kt("k_i", [P, N, 4], BF16, "w2")
+            sl = slice(512 * h + 128 * q, 512 * h + 128 * q + 128)
+            nc.gpsimd.tensor_scalar(
+                out=st["k_i"][:, sl, :], in0=k_sb[:, :, sl].rearrange("p t n -> p n t"),
+                scalar1=1.0, scalar2=0.0, op0=MULT, op1=ADD,
+            )
 
         def qk(h):
             sl = slice(512 * h, 512 * h + 512)
-            nc.vector.quantize_mx(
-                out=k_q[:, sl].bitcast(FP8X4), scales=k_s[:, sl],
-                in_=st["k_i"][:, sl, :].rearrange("p n t -> p (n t)"),
-            )
+            quant(k_q[:, sl], k_s[:, sl], st["k_i"][:, sl, :].rearrange("p n t -> p (n t)"))
 
         def m1(ti):
             pi, j = divmod(ti, 2)
+            cols = slice(128 * j, 128 * j + 128)
             ps = psum_o.tile([P, 512], F32, name="acc")
             for ng in range(2):
-                nc.tensor.matmul_mx(
-                    out=ps[:],
-                    lhsT=x_q[pi][:, ng, 128 * j : 128 * j + 128].bitcast(FP8X4),
-                    lhsT_scale=x_s[pi][:, ng, 128 * j : 128 * j + 128],
-                    rhs=c_q[:, ng, :].bitcast(FP8X4),
-                    rhs_scale=c_s[:, ng, :],
-                    start=(ng == 0), stop=(ng == 1),
-                )
+                mx(ps, x_q[pi][:, ng, cols], x_s[pi][:, ng, cols], c_q[:, ng, :], c_s[:, ng, :], ng == 0, ng == 1)
             st["z", ti] = ps
 
         def nu(ti):
             gi, t = divmod(ti, 4)
-            if ("nu", ti // 2) not in st:
-                st["nu", ti // 2] = ring.tile([P, 2, 512], BF16, name="nu", align_bytes=64, bufs=4)
+            if ti % 2 == 0:
+                st["nu", ti // 2] = rt("nu", [P, 2, 2, 256], BF16, 3)
             nc.vector.tensor_tensor(
-                out=st["nu", ti // 2][:, ti % 2, :].rearrange("p (u w e) -> p u w e", u=2, e=2),
+                out=st["nu", ti // 2][:, :, ti % 2, :].rearrange("p u (w e) -> p u w e", e=2),
                 in0=y_sb[gi][:, t, :].rearrange("p (w u e) -> p u w e", u=2, e=2),
                 in1=st["z", ti][:].rearrange("p (w u e) -> p u w e", u=2, e=2),
                 op=SUB,
             )
 
         def tn(pi):
-            ps = psum_t.tile([P, 512], F32, name="tp")
-            for u in range(2):
-                for j in range(2):
-                    w = words(st["nu", pi][:, j, :])
-                    nc.tensor.transpose(
-                        ps[:, 256 * u + 128 * j : 256 * u + 128 * j + 128], w[:, 128 * u : 128 * u + 128], ident[:]
-                    )
-            st["tn", pi] = ps
+            st["tn", pi] = turn_packed(st["nu", pi][:].rearrange("p u b w -> p (u b w)"))
 
         def en(pi):
-            nt = ring.tile([P, 1024], BF16, name="nt", align_bytes=64, bufs=4)
             nc.scalar.copy(
-                out=nt[:].bitcast(F32).rearrange("p (s u) -> p s u", u=2),
-                in_=st["tn", pi][:].rearrange("p (u s) -> p s u", u=2),
+                out=wout(nt[:, 256 * pi : 256 * pi + 256, :].rearrange("p s t -> p (s t)")), in_=win(st["tn", pi])
             )
-            st["nt", pi] = nt
 
-        def qn(pi):
-            nc.vector.quantize_mx(out=n_q[pi][:].bitcast(FP8X4), scales=n_s[pi][:], in_=st["nt", pi][:])
+        def qn(q):
+            w = 256 * QN
+            sl = slice(w * q, w * q + w)
+            quant(n_q[:, sl], n_s[:, sl], nt[:, sl, :].rearrange("p s t -> p (s t)"))
 
         def ta(ti):
             gi, t = divmod(ti, 4)
             ps = psum_t.tile([P, 512], F32, name="tp")
-            w = words(a_sb[gi][:, t, :])
+            w = a_sb[gi][:, t, :].bitcast(F32)
             for jg in range(2):
                 for u in range(2):
-                    nc.tensor.transpose(
-                        ps[:, 256 * jg + 128 * u : 256 * jg + 128 * u + 128],
-                        w[:, 256 * jg + u : 256 * (jg + 1) : 2],
-                        ident[:],
-                    )
+                    o = 256 * jg + 128 * u
+                    nc.tensor.transpose(ps[:, o : o + 128], w[:, 256 * jg + u : 256 * jg + 256 : 2], ident[:])
             st["ta", ti] = ps
 
         def ea(ti):
-            pi, j = divmod(ti, 2)
-            if ("at", pi) not in st:
-                st["at", pi] = ring.tile([P, 2, 2, 128, 4], BF16, name="at", align_bytes=64, bufs=4)
-            at = st["at", pi]
             nc.scalar.copy(
-                out=at[:, j].rearrange("p j i t -> p (j i t)").bitcast(F32).rearrange("p (j i u) -> p j i u", j=2, u=2),
+                out=at[:, ti].rearrange("p j i t -> p (j i t)").bitcast(F32).rearrange("p (j i u) -> p j i u", j=2, u=2),
                 in_=st["ta", ti][:].rearrange("p (j u i) -> p j i u", j=2, u=2),
             )
 
-        def qa(pi):
-            nc.vector.quantize_mx(
-                out=a_q[pi][:].rearrange("p b j i -> p (b j i)").bitcast(FP8X4),
-                scales=a_s[pi][:].rearrange("p b j i -> p (b j i)"),
-                in_=st["at", pi][:].rearrange("p b j i t -> p (b j i t)"),
+        def qa(q):
+            sl = slice(QA * q, QA * q + QA)
+            quant(
+                a_q[:, sl].rearrange("p b j i -> p (b j i)"), a_s[:, sl].rearrange("p b j i -> p (b j i)"),
+                at[:, sl].rearrange("p b j i t -> p (b j i t)"),
             )
 
-        def deg(pi):
-            ps = psum_o.tile([P, 2], F32, name="acc")
-            for j in range(2):
-                at = st["at", pi][:, j]
+        def dg(q):
+            ps = psum_o.tile([P, DQ], F32, name="acc")
+            for b in range(DQ):
                 for jg in range(2):
                     for t in range(4):
                         nc.tensor.matmul(
-                            ps[:, j : j + 1], at[:, jg, :, t], hg[:, jg, t : t + 1],
+                            ps[:, b : b + 1], at[:, DQ * q + b, jg, :, t], hg[:, jg, t : t + 1],
                             start=(jg == 0 and t == 0), stop=(jg == 1 and t == 3),
                         )
-            st["dg", pi] = ps
+            st["dg", q] = ps
 
-        def ddo(pi):
+        def ddf(q):
             nc.vector.tensor_scalar(
-                out=dd[:, 2 * pi : 2 * pi + 2], in0=st["dg", pi][:], scalar1=-1.0, scalar2=1.0, op0=MULT, op1=ADD
+                out=dd[:, DQ * q : DQ * q + DQ], in0=st["dg", q][:], scalar1=-1.0, scalar2=1.0, op0=MULT, op1=ADD
             )
 
         def m2(ti, h):
-            pi, j = divmod(ti, 2)
-            sl = slice(512 * h, 512 * h + 512)
             ps = psum_o.tile([P, 512], F32, name="acc")
             for jg in range(2):
-                nc.tensor.matmul_mx(
-                    out=ps[:],
-                    lhsT=a_q[pi][:, j, jg, :].bitcast(FP8X4), lhsT_scale=a_s[pi][:, j, jg, :],
-                    rhs=g_q[jg][:, sl].bitcast(FP8X4), rhs_scale=g_s[jg][:, sl],
-                    start=(jg == 0), stop=False,
-                )
-            nc.tensor.matmul_mx(
-                out=ps[:],
-                lhsT=n_q[pi][:, 128 * j : 128 * j + 128].bitcast(FP8X4), lhsT_scale=n_s[pi][:, 128 * j : 128 * j + 128],
-                rhs=k_q[:, sl].bitcast(FP8X4), rhs_scale=k_s[:, sl],
-                start=False, stop=True,
-            )
+                mx(ps, a_q[:, ti, jg, :], a_s[:, ti, jg, :], g_q[h][:, jg, :], g_s[h][:, jg, :], jg == 0, False)
+            rows, cols = slice(128 * ti, 128 * ti + 128), slice(512 * h, 512 * h + 512)
+            mx(ps, n_q[:, rows], n_s[:, rows], k_q[:, cols], k_s[:, cols], False, True)
             st["m2", ti, h] = ps
-
-        def stt(ti, h):
-            gi, t = divmod(ti, 4)
-            o = ring.tile([P, 512], F32, name="o", align_bytes=64, bufs=8)
-            st["o", ti, h] = o
-            nc.vector.scalar_tensor_tensor(
-                out=o[:], in0=x_sb[gi][:, t, 512 * h : 512 * h + 512], scalar=dd[:, ti : ti + 1],
-                in1=st["m2", ti, h][:], op0=MULT, op1=ADD,
-            )
 
         out_r = out_0.rearrange("(g p t) n -> g p t n", g=2, t=4)
 
-        def so(ti, h):
+        def stt(ti, h):
             gi, t = divmod(ti, 4)
-            nc.sync.dma_start(out=out_r[gi, :, t, 512 * h : 512 * h + 512], in_=st["o", ti, h][:])
+            if ti % 2 == 0:
+                st["o", ti // 2, h] = rt("o", [P, 2, 512], F32, 5)
+            cols = slice(512 * h, 512 * h + 512)
+            o = st["o", ti // 2, h][:, ti % 2, :]
+            nc.vector.scalar_tensor_tensor(
+                out=o, in0=x_sb[gi][:, t, cols], scalar=dd[:, ti : ti + 1], in1=st["m2", ti, h][:], op0=MULT, op1=ADD
+            )
+            nc.sync.dma_start(out=out_r[gi, :, t, cols], in_=o)
 
-        def rd(ti, h):
-            if ("ob", ti // 2, h) not in st:
-                st["ob", ti // 2, h] = ring.tile([P, 2, 512], BF16, name="ob", align_bytes=64, bufs=5)
-            dst = st["ob", ti // 2, h][:, ti % 2, :].rearrange("p (u w e) -> p u w e", u=2, e=2)
-            src = st["o", ti, h][:].rearrange("p (w u e) -> p u w e", u=2, e=2)
-            e = RENG[ti + 8 * h]
-            if e == "G":
-                nc.gpsimd.tensor_scalar(out=dst, in0=src, scalar1=1.0, scalar2=0.0, op0=MULT, op1=ADD)
-            elif e == "V":
-                nc.vector.tensor_copy(out=dst, in_=src)
+        def rd(pi, h, tile=None):
+            if ("ob", pi, h) not in st:
+                st["ob", pi, h] = rt("ob", [P, 2, 2, 256], BF16, 4)
+            ob, o = st["ob", pi, h], st["o", pi, h]
+            if tile is None:
+                nc.scalar.copy(
+                    out=ob[:].rearrange("p u b (w e) -> p u (b w) e", e=2),
+                    in_=o[:].rearrange("p b (w u e) -> p u (b w) e", u=2, e=2),
+                )
             else:
-                nc.scalar.copy(out=dst, in_=src)
-
-        def to(pi, h):
-            ps = psum_t.tile([P, 512], F32, name="tp")
-            for u in range(2):
-                for j in range(2):
-                    w = words(st["ob", pi, h][:, j, :])
-                    nc.tensor.transpose(
-                        ps[:, 256 * u + 128 * j : 256 * u + 128 * j + 128], w[:, 128 * u : 128 * u + 128], ident[:]
-                    )
-            st["to", pi, h] = ps
-
-        def eo(pi, h):
-            gi, hf = divmod(pi, 2)
-            if ("o_t", h) not in st:
-                st["o_t", h] = keep.tile([P, 2, 512, 4], BF16, name="o_t%d" % h, tag="w%d" % h, align_bytes=64)
-            dst = st["o_t", h][:, gi].rearrange("p i t -> p (i t)").bitcast(F32).rearrange("p (i t u) -> p i t u", t=4, u=2)
-            nc.scalar.copy(
-                out=dst[:, :, 2 * hf : 2 * hf + 2, :],
-                in_=st["to", pi, h][:].rearrange("p (u t i) -> p i t u", u=2, t=2),
-            )
-
-        def qo(gi, h):
-            nc.vector.quantize_mx(
-                out=o_q[h][gi][:].bitcast(FP8X4), scales=o_s[h][gi][:], in_=st["o_t", h][:, gi].rearrange("p i t -> p (i t)")
-            )
-            nc.sync.dma_start(
-                out=out_1[h, :, 512 * gi : 512 * gi + 512, :].rearrange("p m t -> p (m t)").bitcast(I32),
-                in_=o_q[h][gi][:].bitcast(I32),
-            )
-            for q in range(4):
-                nc.scalar.dma_start(
-                    out=out_2[h, 4 * q : 4 * q + 4, 512 * gi : 512 * gi + 512].bitcast(I32),
-                    in_=o_s[h][gi][32 * q : 32 * q + 4, :].bitcast(I32),
+                fn = nc.vector.tensor_copy if (pi, h) == (3, 1) else nc.scalar.copy
+                fn(
+                    out=ob[:, :, tile, :].rearrange("p u (w e) -> p u w e", e=2),
+                    in_=o[:, tile, :].rearrange("p (w u e) -> p u w e", u=2, e=2),
                 )
 
+        def to(pi, h):
+            st["to", pi, h] = turn_packed(st["ob", pi, h][:].rearrange("p u b w -> p (u b w)"))
+
+        def eo(pi, h, r=slice(0, 128)):
+            gi, hf = divmod(pi, 2)
+            if ("ot", h) not in st:
+                st["ot", h] = kt("o_t%d" % h, [P, 2, 512, 4], BF16, "w%d" % h)
+            dst = st["ot", h][:, gi].rearrange("p i t -> p (i t)").bitcast(F32).rearrange("p (i t u) -> p i t u", t=4, u=2)
+            nc.scalar.copy(
+                out=dst[:, r, 2 * hf : 2 * hf + 2, :],
+                in_=st["to", pi, h][:].rearrange("p (u t i) -> p i t u", u=2, t=2)[:, r],
+            )
+
+        def qo(gi, h, i0=0, w=512):
+            r = slice(i0, i0 + w)
+            quant(o_q[h][gi][:, r], o_s[h][gi][:, r], st["ot", h][:, gi, r, :].rearrange("p i t -> p (i t)"))
+            nc.sync.dma_start(
+                out=out_1[h, :, 512 * gi + i0 : 512 * gi + i0 + w, :].rearrange("p m t -> p (m t)").bitcast(I32),
+                in_=o_q[h][gi][:, r].bitcast(I32),
+            )
+            if i0 + w == 512:
+                for q in range(4):
+                    (nc.scalar if q % 2 else nc.sync).dma_start(
+                        out=out_2[h, 4 * q : 4 * q + 4, 512 * gi : 512 * gi + 512].bitcast(I32),
+                        in_=o_s[h][gi][32 * q : 32 * q + 4, :].bitcast(I32),
+                    )
 
         def run(n):
-            d = [int(z) for z in n if z in "0123456789"]
+            d = [int(z) for z in n[2:] if z in "0123456789"]
             f = n[:2]
-            if f == "tx":
-                tx(d[0], d[1])
-            elif f == "xp":
-                xp(d[0], d[1])
-            elif f == "qx":
-                qx(d[0])
-            elif f == "mu":
-                mu(d[0], d[1])
-            elif f == "tc":
-                tcc(d[0], d[1])
-            elif f == "ec":
-                ec(d[0], d[1])
+            table = {"tx": tx, "xp": xp, "qx": qx, "tc": tcc, "ec": ec, "mu": mu, "il": il, "qg": qg, "ki": ki, "qk": qk,
+                     "m1": m1, "nu": nu, "tn": tn, "en": en, "qn": qn, "ta": ta, "ea": ea, "qa": qa, "dg": dg, "dd": ddf,
+                     "m2": m2, "st": stt, "to": to}
+            if f in table:
+                table[f](*d)
             elif f == "qc":
-                qc(d[0])
-            elif f == "il":
-                il(d[0], d[1], d[2])
-            elif f == "qg":
-                qg(d[0], d[1])
-            elif f == "ki":
-                ki(d[0], d[1], KENG[d[0]])
-            elif f == "qk":
-                qk(d[0])
-            elif f == "m1":
-                m1(d[1])
-            elif f == "nu":
-                nu(d[0])
-            elif f == "ta":
-                ta(d[0])
-            elif f == "ea":
-                ea(d[0])
-            elif f == "qa":
-                qa(d[0])
-            elif f == "tn":
-                tn(d[0])
-            elif f == "en":
-                en(d[0])
-            elif f == "qn":
-                qn(d[0])
-            elif f == "dg":
-                deg(d[0])
-            elif f == "dd":
-                ddo(d[0])
-            elif f == "m2":
-                m2(d[1], d[2])
-            elif f == "st":
-                stt(d[0], d[1])
-                so(d[0], d[1])
+                qc()
             elif f == "rd":
-                rd(d[0], d[1])
-            elif f == "to":
-                to(d[0], d[1])
+                if RP:
+                    rd(d[0], d[1])
+                else:
+                    rd(d[0] // 2, d[1], d[0] % 2)
+            elif f == "rv":
+                rd(3, 1, d[0] - 6)
+            elif n == "eo31":
+                eo(3, 1, slice(0, 64))
+            elif n == "fo31":
+                eo(3, 1, slice(64, 128))
             elif f == "eo":
                 eo(d[0], d[1])
+            elif n == "qp11":
+                qo(1, 1, 0, 256)
+            elif n == "qo11":
+                qo(1, 1, 256, 256)
             elif f == "qo":
                 qo(d[0], d[1])
 

@@ -18,16 +18,20 @@ SUB = mybir.AluOpType.subtract
 COPY = mybir.ActivationFunctionType.Copy
 
 P = 128
-MENG = "SSSVVVVV"
-QA, QN, DQ, RP = 4, 2, 4, 1
-ORDER = "tx00 mu00 tx01 xp00 mu01 xp01 mu02 tx10 tx11 xp10 xp11 tc00 tc01 ec00 tc10 ec01 ki00 qx0 mu03 ki01 mu10 ec10 qx1 mu11 tc11 tx20 ec11 tx21 qc0 il00 tx30 mu12 mu13 tx31 m1_0 xp20 il10 xp21 m1_1 m1_2 xp30 ta0 qx2 ta1 ta2 nu0 m1_3 ki02 nu1 xp31 ki03 m1_4 ki10 nu2 ea0 ta3 ea1 tn0 nu3 ta4 ea2 m1_5 tn1 ea3 qx3 qk0 ta5 en0 qa0 ki11 ea4 ta6 nu4 en1 m1_6 ea5 dg0 qg0 nu5 m1_7 ta7 dd0 ki12 qn0 nu6 il01 nu7 ea6 tn2 en2 ea7 m2_00 m2_10 ki13 tn3 dg1 st00 en3 m2_20 m2_30 qk1 il11 qa1 qn1 dd1 st10 st20 st30 m2_40 st40 rd00 m2_50 qg1 rd10 st50 m2_60 to00 m2_70 st60 eo00 st70 m2_01 st01 rd20 m2_11 m2_21 m2_31 st11 rd30 to10 rd01 st21 to20 to30 st31 eo10 eo20 m2_41 qo00 eo30 m2_51 st41 m2_61 rd11 st51 m2_71 st61 to01 to11 rd21 st71 rv6 rv7 eo01 to21 eo11 to31 qo10 eo21 qo01 eo31 fo31 qp11 qo11"
+NS = 3
+QUEUES = (
+    "tx*4 tc*4 tx*4 m1*4 ta tn ta*2 m1 ta tn ta*2 m1 dg m1*2 ta*2 tn m2*2 tn dg m2*6 to*2 m2*4 to*2 m2*4 to*4",
+    "xp*3 qx xp mv qx mv*2 xp qc xp mv*2 xp nu*2 xp qx nu*2 qg qx nu qk qn nu qa dd nu*2 qk st qa qn dd st*5 qg st*5 qo st*3 qo st*2 rv*2 qo*3",
+    "ms*3 ec*4 il*2 ea*3 en ea en ea*2 il ea*2 en*2 il rd*3 eo rd eo rd eo*2 rd*2 eo*5",
+    "ki*8",
+)
 
 
 def tile_signedkalmanconsensusfilterstep_x1_kernel(tc, x, y, p, c, k, a, g, out_0, out_1, out_2):
     nc = tc.nc
     with ExitStack() as ctx:
         keep = ctx.enter_context(tc.tile_pool(name="keep", bufs=1))
-        ring = ctx.enter_context(tc.tile_pool(name="ring", bufs=4))
+        ring = ctx.enter_context(tc.tile_pool(name="ring", bufs=1))
         psum_t = ctx.enter_context(tc.psum_pool(name="psum_t", bufs=4))
         psum_o = ctx.enter_context(tc.psum_pool(name="psum_o", bufs=4))
 
@@ -43,27 +47,29 @@ def tile_signedkalmanconsensusfilterstep_x1_kernel(tc, x, y, p, c, k, a, g, out_
         hg = kt("hg", [P, 2, 4], BF16)
         hgf = kt("hgf", [P, 2, 4], F32)
         dd = kt("dd", [P, 8], F32)
-        x_sb = [kt("x_sb%d" % i, [P, 4, N], BF16) for i in range(2)]
-        a_sb = [kt("a_sb%d" % i, [P, 4, S], BF16) for i in range(2)]
-        y_sb = [kt("y_sb%d" % i, [P, 4, M], BF16) for i in range(2)]
+        x_sb = kt("x_sb", [P, 8, N], BF16)
+        a_sb = kt("a_sb", [P, 8, S], BF16)
+        y_sb = kt("y_sb", [P, 8, M], BF16)
         c_sb = kt("c_sb", [P, 4, N], BF16, "w0")
         k_sb = kt("k_sb", [P, 4, N], BF16, "w1")
         c_t = kt("c_t", [P, 2, M, 4], BF16, "w2")
+        k_i = kt("k_i", [P, N, 4], BF16, "w2")
+        o_t = [kt("o_t%d" % h, [P, S, 4], BF16, "w%d" % h) for h in range(2)]
+        xm = kt("xm", [P, 8, N], BF16)
         c_q = kt("c_q", [P, 2, M], U32)
         c_s = kt("c_s", [P, 2, M], U8)
         k_q = kt("k_q", [P, N], U32)
         k_s = kt("k_s", [P, N], U8)
-        xm = [kt("xm%d" % i, [P, 4, N], BF16) for i in range(2)]
-        g_q = [kt("g_q%d" % i, [P, 2, 512], U32) for i in range(2)]
-        g_s = [kt("g_s%d" % i, [P, 2, 512], U8) for i in range(2)]
-        x_q = [kt("x_q%d" % i, [P, 2, 256], U32) for i in range(4)]
-        x_s = [kt("x_s%d" % i, [P, 2, 256], U8) for i in range(4)]
+        g_q = kt("g_q", [P, 2, 2, 512], U32)
+        g_s = kt("g_s", [P, 2, 2, 512], U8)
+        x_q = kt("x_q", [P, 4, 2, 256], U32)
+        x_s = kt("x_s", [P, 4, 2, 256], U8)
         n_q = kt("n_q", [P, S], U32)
         n_s = kt("n_s", [P, S], U8)
         a_q = kt("a_q", [P, 8, 2, P], U32)
         a_s = kt("a_s", [P, 8, 2, P], U8)
-        o_q = [[kt("o_q%d%d" % (i, j), [P, 512], U32) for j in range(2)] for i in range(2)]
-        o_s = [[kt("o_s%d%d" % (i, j), [P, 512], U8) for j in range(2)] for i in range(2)]
+        o_q = [kt("o_q%d" % h, [P, S], U32) for h in range(2)]
+        o_s = [kt("o_s%d" % h, [P, S], U8) for h in range(2)]
         nt = kt("nt", [P, S, 4], BF16)
         at = kt("at", [P, 8, 2, P, 4], BF16)
 
@@ -75,43 +81,52 @@ def tile_signedkalmanconsensusfilterstep_x1_kernel(tc, x, y, p, c, k, a, g, out_
         yr = y.rearrange("(g p t) n -> g p t n", g=2, t=4)
         cr = c.rearrange("(b p) n -> p b n", p=P)
         kr = k.rearrange("(p t) n -> p t n", t=4)
-        lo, hi = slice(0, 2), slice(2, 4)
-        for t in range(2):
-            nc.sync.dma_start(out=x_sb[0][:, t, :], in_=xr[0, :, t, :])
-        nc.sync.dma_start(out=x_sb[0][:, hi, :], in_=xr[0, :, hi, :])
-        nc.sync.dma_start(out=c_sb[:, lo, :], in_=cr[:, lo, :])
-        nc.sync.dma_start(out=c_sb[:, hi, :], in_=cr[:, hi, :])
-        nc.sync.dma_start(out=x_sb[1][:, lo, :], in_=xr[1, :, lo, :])
-        nc.sync.dma_start(out=x_sb[1][:, hi, :], in_=xr[1, :, hi, :])
-        nc.sync.dma_start(out=y_sb[0][:], in_=yr[0])
-        nc.sync.dma_start(out=k_sb[:, :, 0:512], in_=kr[:, :, 0:512])
-        nc.sync.dma_start(out=a_sb[0][:, lo, :], in_=ar[0, :, lo, :])
-        nc.sync.dma_start(out=a_sb[0][:, hi, :], in_=ar[0, :, hi, :])
-        nc.sync.dma_start(out=k_sb[:, :, 512:1024], in_=kr[:, :, 512:1024])
-        nc.sync.dma_start(out=a_sb[1][:, lo, :], in_=ar[1, :, lo, :])
-        nc.sync.dma_start(out=y_sb[1][:], in_=yr[1])
-        nc.sync.dma_start(out=a_sb[1][:, hi, :], in_=ar[1, :, hi, :])
+
+        def load(dst, src, rows, cols):
+            nc.sync.dma_start(out=dst[:, rows, cols], in_=src[:, slice(rows.start % 4, rows.start % 4 + rows.stop - rows.start), cols])
+
+        whole, left, right = slice(0, 1024), slice(0, 512), slice(512, 1024)
+        load(x_sb, xr[0], slice(0, 2), left)
+        load(x_sb, xr[0], slice(0, 2), right)
+        load(x_sb, xr[0], slice(2, 4), whole)
+        load(c_sb, cr, slice(0, 2), whole)
+        load(c_sb, cr, slice(2, 4), whole)
+        load(x_sb, xr[1], slice(4, 6), whole)
+        load(x_sb, xr[1], slice(6, 8), whole)
+        load(y_sb, yr[0], slice(0, 4), left)
+        load(k_sb, kr, slice(0, 4), left)
+        load(a_sb, ar[0], slice(0, 2), whole)
+        load(a_sb, ar[0], slice(2, 4), whole)
+        load(k_sb, kr, slice(0, 4), right)
+        load(a_sb, ar[1], slice(4, 6), whole)
+        load(y_sb, yr[1], slice(4, 8), left)
+        load(a_sb, ar[1], slice(6, 8), whole)
         nc.vector.tensor_scalar_mul(hgf[:], g_t[:], 0.5)
         nc.vector.tensor_scalar_mul(hg[:], g_t[:], 0.5)
 
         st = {}
+        steps = {}
 
-        def turn(rows, col):
-            ps = psum_t.tile([P, 512], F32, name="tp")
+        def add(kind, action, *needs):
+            steps.setdefault(kind, []).append((action, needs))
+
+        def bank(pool, width=512):
+            return pool.tile([P, width], F32, name="bank")
+
+        def turn_rows(tiles, ng):
+            ps = bank(psum_t)
             for u in range(2):
                 for j in range(2):
-                    nc.tensor.transpose(
-                        ps[:, 256 * u + 128 * j : 256 * u + 128 * j + 128], rows[j].bitcast(F32)[:, col(u)], ident[:]
-                    )
+                    words = tiles[:, j, :].bitcast(F32)
+                    o = 256 * u + 128 * j
+                    nc.tensor.transpose(ps[:, o : o + 128], words[:, 256 * ng + u : 256 * ng + 256 : 2], ident[:])
             return ps
 
-        def every2(ng):
-            return lambda u: slice(256 * ng + u, 256 * ng + 256, 2)
-
         def turn_packed(src):
-            ps = psum_t.tile([P, 512], F32, name="tp")
+            ps = bank(psum_t)
+            words = src.rearrange("p u b w -> p (u b w)").bitcast(F32)
             for o in range(0, 512, 128):
-                nc.tensor.transpose(ps[:, o : o + 128], src.bitcast(F32)[:, o : o + 128], ident[:])
+                nc.tensor.transpose(ps[:, o : o + 128], words[:, o : o + 128], ident[:])
             return ps
 
         def wout(ap):
@@ -128,109 +143,144 @@ def tile_signedkalmanconsensusfilterstep_x1_kernel(tc, x, y, p, c, k, a, g, out_
                 out=ps[:], lhsT=lq.bitcast(FP8X4), lhsT_scale=ls, rhs=rq.bitcast(FP8X4), rhs_scale=rs, start=first, stop=last
             )
 
-        def tx(pi, ng):
-            gi, hf = divmod(pi, 2)
-            st["tx", pi, ng] = turn([x_sb[gi][:, 2 * hf + j, :] for j in range(2)], every2(ng))
+        def tx(i):
+            pi, ng = divmod(i, 2)
+            st["tx", i] = turn_rows(x_sb[:, 2 * pi : 2 * pi + 2, :], ng)
 
-        def xp(pi, ng):
+        def xp(i):
+            pi, ng = divmod(i, 2)
             if ng == 0:
                 st["xt", pi] = rt("xt", [P, 2, 1024], BF16, 3)
             nc.vector.tensor_tensor(
                 out=st["xt", pi][:, ng, :].rearrange("p (s u e) -> p s u e", u=2, e=2),
-                in0=st["tx", pi, ng][:].bitcast(BF16).rearrange("p (u s e) -> p s u e", u=2, e=2),
+                in0=st["tx", i][:].bitcast(BF16).rearrange("p (u s e) -> p s u e", u=2, e=2),
                 in1=p_t[:, ng, :].rearrange("p (u e) -> p u e", e=2).unsqueeze(1).broadcast_to([P, 256, 2, 2]),
                 op=MULT,
             )
 
-        def qx(pi):
+        def qx(i):
             quant(
-                x_q[pi][:].rearrange("p n s -> p (n s)"), x_s[pi][:].rearrange("p n s -> p (n s)"),
-                st["xt", pi][:].rearrange("p n s -> p (n s)"),
+                x_q[:, i].rearrange("p n s -> p (n s)"), x_s[:, i].rearrange("p n s -> p (n s)"),
+                st["xt", i][:].rearrange("p n s -> p (n s)"),
             )
 
-        def tcc(b, ng):
-            st["tc", b, ng] = turn([c_sb[:, 2 * b + j, :] for j in range(2)], every2(ng))
+        for i in range(8):
+            add("tx", lambda i=i: tx(i))
+            add("xp", lambda i=i: xp(i), ("tx", i))
+        for i in range(4):
+            add("qx", lambda i=i: qx(i), ("xp", 2 * i + 1))
 
-        def ec(b, ng):
-            nc.scalar.copy(
-                out=wout(c_t[:, ng, 256 * b : 256 * b + 256, :].rearrange("p m t -> p (m t)")), in_=win(st["tc", b, ng])
-            )
+        def tcc(i):
+            b, ng = divmod(i, 2)
+            st["tc", i] = turn_rows(c_sb[:, 2 * b : 2 * b + 2, :], ng)
+
+        def ec(i):
+            b, ng = divmod(i, 2)
+            cols = slice(256 * b, 256 * b + 256)
+            nc.scalar.copy(out=wout(c_t[:, ng, cols, :].rearrange("p m t -> p (m t)")), in_=win(st["tc", i]))
 
         def qc():
-            quant(c_q[:].rearrange("p n m -> p (n m)"), c_s[:].rearrange("p n m -> p (n m)"), c_t[:].rearrange("p n m t -> p (n m t)"))
+            quant(
+                c_q[:].rearrange("p n m -> p (n m)"), c_s[:].rearrange("p n m -> p (n m)"),
+                c_t[:].rearrange("p n m t -> p (n m t)"),
+            )
 
-        def mu(gi, t):
-            if MENG[4 * gi + t] == "S":
-                nc.scalar.activation(out=xm[gi][:, t, :], in_=x_sb[gi][:, t, :], func=COPY, scale=hgf[:, gi, t : t + 1])
+        for i in range(4):
+            add("tc", lambda i=i: tcc(i))
+            add("ec", lambda i=i: ec(i), ("tc", i))
+        add("qc", qc, ("ec", 3))
+
+        def mu(ti, eng):
+            gi, t = divmod(ti, 4)
+            sc = hgf[:, gi, t : t + 1]
+            if eng == "S":
+                nc.scalar.activation(out=xm[:, ti, :], in_=x_sb[:, ti, :], func=COPY, scale=sc)
             else:
-                nc.vector.tensor_scalar_mul(xm[gi][:, t, :], x_sb[gi][:, t, :], hgf[:, gi, t : t + 1])
+                nc.vector.tensor_scalar_mul(xm[:, ti, :], x_sb[:, ti, :], sc)
 
-        def il(gi, h):
+        def il(i):
+            h, gi = divmod(i, 2)
             if gi == 0:
                 st["xi", h] = rt("xi", [P, 2, 512, 4], BF16, 2)
-            nc.scalar.copy(
-                out=st["xi", h][:, gi], in_=xm[gi][:, :, 512 * h : 512 * h + 512].rearrange("p t n -> p n t")
-            )
+            cols = slice(512 * h, 512 * h + 512)
+            nc.scalar.copy(out=st["xi", h][:, gi], in_=xm[:, 4 * gi : 4 * gi + 4, cols].rearrange("p t n -> p n t"))
 
         def qg(h):
             quant(
-                g_q[h][:].rearrange("p g n -> p (g n)"), g_s[h][:].rearrange("p g n -> p (g n)"),
+                g_q[:, h].rearrange("p g n -> p (g n)"), g_s[:, h].rearrange("p g n -> p (g n)"),
                 st["xi", h][:].rearrange("p g n t -> p (g n t)"),
             )
 
-        def ki(h, q):
-            if (h, q) == (0, 0):
-                st["k_i"] = kt("k_i", [P, N, 4], BF16, "w2")
-            sl = slice(512 * h + 128 * q, 512 * h + 128 * q + 128)
+        for ti in range(NS):
+            add("ms", lambda ti=ti: mu(ti, "S"))
+        for ti in range(NS, 8):
+            add("mv", lambda ti=ti: mu(ti, "V"))
+        for i in range(4):
+            add("il", lambda i=i: il(i), *((("mv", 7 - NS),) if i % 2 else (("ms", min(NS, 4) - 1), ("mv", 3 - NS))))
+        for h in range(2):
+            add("qg", lambda h=h: qg(h), ("il", 2 * h + 1))
+
+        def ki(i):
+            cols = slice(128 * i, 128 * i + 128)
             nc.gpsimd.tensor_scalar(
-                out=st["k_i"][:, sl, :], in0=k_sb[:, :, sl].rearrange("p t n -> p n t"),
+                out=k_i[:, cols, :], in0=k_sb[:, :, cols].rearrange("p t n -> p n t"),
                 scalar1=1.0, scalar2=0.0, op0=MULT, op1=ADD,
             )
 
         def qk(h):
-            sl = slice(512 * h, 512 * h + 512)
-            quant(k_q[:, sl], k_s[:, sl], st["k_i"][:, sl, :].rearrange("p n t -> p (n t)"))
+            cols = slice(512 * h, 512 * h + 512)
+            quant(k_q[:, cols], k_s[:, cols], k_i[:, cols, :].rearrange("p n t -> p (n t)"))
+
+        for i in range(8):
+            add("ki", lambda i=i: ki(i), ("qc", 0))
+        for h in range(2):
+            add("qk", lambda h=h: qk(h), ("ki", 4 * h + 3))
 
         def m1(ti):
             pi, j = divmod(ti, 2)
             cols = slice(128 * j, 128 * j + 128)
-            ps = psum_o.tile([P, 512], F32, name="acc")
+            ps = bank(psum_o)
             for ng in range(2):
-                mx(ps, x_q[pi][:, ng, cols], x_s[pi][:, ng, cols], c_q[:, ng, :], c_s[:, ng, :], ng == 0, ng == 1)
-            st["z", ti] = ps
+                mx(ps, x_q[:, pi, ng, cols], x_s[:, pi, ng, cols], c_q[:, ng, :], c_s[:, ng, :], ng == 0, ng == 1)
+            st["m1", ti] = ps
 
         def nu(ti):
-            gi, t = divmod(ti, 4)
             if ti % 2 == 0:
                 st["nu", ti // 2] = rt("nu", [P, 2, 2, 256], BF16, 3)
             nc.vector.tensor_tensor(
                 out=st["nu", ti // 2][:, :, ti % 2, :].rearrange("p u (w e) -> p u w e", e=2),
-                in0=y_sb[gi][:, t, :].rearrange("p (w u e) -> p u w e", u=2, e=2),
-                in1=st["z", ti][:].rearrange("p (w u e) -> p u w e", u=2, e=2),
+                in0=y_sb[:, ti, :].rearrange("p (w u e) -> p u w e", u=2, e=2),
+                in1=st["m1", ti][:].rearrange("p (w u e) -> p u w e", u=2, e=2),
                 op=SUB,
             )
 
         def tn(pi):
-            st["tn", pi] = turn_packed(st["nu", pi][:].rearrange("p u b w -> p (u b w)"))
+            st["tn", pi] = turn_packed(st["nu", pi][:])
 
         def en(pi):
-            nc.scalar.copy(
-                out=wout(nt[:, 256 * pi : 256 * pi + 256, :].rearrange("p s t -> p (s t)")), in_=win(st["tn", pi])
-            )
+            rows = slice(256 * pi, 256 * pi + 256)
+            nc.scalar.copy(out=wout(nt[:, rows, :].rearrange("p s t -> p (s t)")), in_=win(st["tn", pi]))
 
-        def qn(q):
-            w = 256 * QN
-            sl = slice(w * q, w * q + w)
-            quant(n_q[:, sl], n_s[:, sl], nt[:, sl, :].rearrange("p s t -> p (s t)"))
+        def qn(i):
+            rows = slice(512 * i, 512 * i + 512)
+            quant(n_q[:, rows], n_s[:, rows], nt[:, rows, :].rearrange("p s t -> p (s t)"))
+
+        for ti in range(8):
+            add("m1", lambda ti=ti: m1(ti), ("qx", ti // 2), ("qc", 0))
+            add("nu", lambda ti=ti: nu(ti), ("m1", ti))
+        for pi in range(4):
+            add("tn", lambda pi=pi: tn(pi), ("nu", 2 * pi + 1))
+            add("en", lambda pi=pi: en(pi), ("tn", pi))
+        for i in range(2):
+            add("qn", lambda i=i: qn(i), ("en", 2 * i + 1))
 
         def ta(ti):
-            gi, t = divmod(ti, 4)
-            ps = psum_t.tile([P, 512], F32, name="tp")
-            w = a_sb[gi][:, t, :].bitcast(F32)
+            ps = bank(psum_t)
+            words = a_sb[:, ti, :].bitcast(F32)
             for jg in range(2):
                 for u in range(2):
                     o = 256 * jg + 128 * u
-                    nc.tensor.transpose(ps[:, o : o + 128], w[:, 256 * jg + u : 256 * jg + 256 : 2], ident[:])
+                    nc.tensor.transpose(ps[:, o : o + 128], words[:, 256 * jg + u : 256 * jg + 256 : 2], ident[:])
             st["ta", ti] = ps
 
         def ea(ti):
@@ -239,123 +289,151 @@ def tile_signedkalmanconsensusfilterstep_x1_kernel(tc, x, y, p, c, k, a, g, out_
                 in_=st["ta", ti][:].rearrange("p (j u i) -> p j i u", j=2, u=2),
             )
 
-        def qa(q):
-            sl = slice(QA * q, QA * q + QA)
+        def qa(i):
+            tl = slice(4 * i, 4 * i + 4)
             quant(
-                a_q[:, sl].rearrange("p b j i -> p (b j i)"), a_s[:, sl].rearrange("p b j i -> p (b j i)"),
-                at[:, sl].rearrange("p b j i t -> p (b j i t)"),
+                a_q[:, tl].rearrange("p b j i -> p (b j i)"), a_s[:, tl].rearrange("p b j i -> p (b j i)"),
+                at[:, tl].rearrange("p b j i t -> p (b j i t)"),
             )
 
-        def dg(q):
-            ps = psum_o.tile([P, DQ], F32, name="acc")
-            for b in range(DQ):
+        def dg(i):
+            ps = bank(psum_o, 4)
+            for b in range(4):
                 for jg in range(2):
                     for t in range(4):
                         nc.tensor.matmul(
-                            ps[:, b : b + 1], at[:, DQ * q + b, jg, :, t], hg[:, jg, t : t + 1],
+                            ps[:, b : b + 1], at[:, 4 * i + b, jg, :, t], hg[:, jg, t : t + 1],
                             start=(jg == 0 and t == 0), stop=(jg == 1 and t == 3),
                         )
-            st["dg", q] = ps
+            st["dg", i] = ps
 
-        def ddf(q):
+        def ddf(i):
             nc.vector.tensor_scalar(
-                out=dd[:, DQ * q : DQ * q + DQ], in0=st["dg", q][:], scalar1=-1.0, scalar2=1.0, op0=MULT, op1=ADD
+                out=dd[:, 4 * i : 4 * i + 4], in0=st["dg", i][:], scalar1=-1.0, scalar2=1.0, op0=MULT, op1=ADD
             )
 
-        def m2(ti, h):
-            ps = psum_o.tile([P, 512], F32, name="acc")
+        for ti in range(8):
+            add("ta", lambda ti=ti: ta(ti))
+            add("ea", lambda ti=ti: ea(ti), ("ta", ti))
+        for i in range(2):
+            add("qa", lambda i=i: qa(i), ("ea", 4 * i + 3))
+            add("dg", lambda i=i: dg(i), ("ea", 4 * i + 3))
+            add("dd", lambda i=i: ddf(i), ("dg", i))
+
+        def m2(i):
+            h, ti = divmod(i, 8)
+            ps = bank(psum_o)
             for jg in range(2):
-                mx(ps, a_q[:, ti, jg, :], a_s[:, ti, jg, :], g_q[h][:, jg, :], g_s[h][:, jg, :], jg == 0, False)
+                mx(ps, a_q[:, ti, jg, :], a_s[:, ti, jg, :], g_q[:, h, jg, :], g_s[:, h, jg, :], jg == 0, False)
             rows, cols = slice(128 * ti, 128 * ti + 128), slice(512 * h, 512 * h + 512)
             mx(ps, n_q[:, rows], n_s[:, rows], k_q[:, cols], k_s[:, cols], False, True)
-            st["m2", ti, h] = ps
+            st["m2", i] = ps
 
-        out_r = out_0.rearrange("(g p t) n -> g p t n", g=2, t=4)
+        out_r = out_0.rearrange("(g p t) n -> p g t n", g=2, t=4)
 
-        def stt(ti, h):
+        def stt(i):
+            h, ti = divmod(i, 8)
             gi, t = divmod(ti, 4)
-            if ti % 2 == 0:
-                st["o", ti // 2, h] = rt("o", [P, 2, 512], F32, 5)
+            if i % 2 == 0:
+                st["o", i // 2] = rt("o", [P, 2, 512], F32, 5)
             cols = slice(512 * h, 512 * h + 512)
-            o = st["o", ti // 2, h][:, ti % 2, :]
+            o = st["o", i // 2][:, i % 2, :]
             nc.vector.scalar_tensor_tensor(
-                out=o, in0=x_sb[gi][:, t, cols], scalar=dd[:, ti : ti + 1], in1=st["m2", ti, h][:], op0=MULT, op1=ADD
+                out=o, in0=x_sb[:, ti, cols], scalar=dd[:, ti : ti + 1], in1=st["m2", i][:], op0=MULT, op1=ADD
             )
-            nc.sync.dma_start(out=out_r[gi, :, t, cols], in_=o)
+            if i % 2:
+                nc.sync.dma_start(out=out_r[:, gi, t - 1 : t + 1, cols], in_=st["o", i // 2][:])
 
-        def rd(pi, h, tile=None):
-            if ("ob", pi, h) not in st:
-                st["ob", pi, h] = rt("ob", [P, 2, 2, 256], BF16, 4)
-            ob, o = st["ob", pi, h], st["o", pi, h]
-            if tile is None:
-                nc.scalar.copy(
-                    out=ob[:].rearrange("p u b (w e) -> p u (b w) e", e=2),
-                    in_=o[:].rearrange("p b (w u e) -> p u (b w) e", u=2, e=2),
-                )
-            else:
-                fn = nc.vector.tensor_copy if (pi, h) == (3, 1) else nc.scalar.copy
-                fn(
-                    out=ob[:, :, tile, :].rearrange("p u (w e) -> p u w e", e=2),
-                    in_=o[:, tile, :].rearrange("p (w u e) -> p u w e", u=2, e=2),
-                )
-
-        def to(pi, h):
-            st["to", pi, h] = turn_packed(st["ob", pi, h][:].rearrange("p u b w -> p (u b w)"))
-
-        def eo(pi, h, r=slice(0, 128)):
-            gi, hf = divmod(pi, 2)
-            if ("ot", h) not in st:
-                st["ot", h] = kt("o_t%d" % h, [P, 2, 512, 4], BF16, "w%d" % h)
-            dst = st["ot", h][:, gi].rearrange("p i t -> p (i t)").bitcast(F32).rearrange("p (i t u) -> p i t u", t=4, u=2)
+        def rd(i):
+            st["ob", i] = rt("ob", [P, 2, 2, 256], BF16, 4)
             nc.scalar.copy(
-                out=dst[:, r, 2 * hf : 2 * hf + 2, :],
-                in_=st["to", pi, h][:].rearrange("p (u t i) -> p i t u", u=2, t=2)[:, r],
+                out=st["ob", i][:].rearrange("p u b (w e) -> p u (b w) e", e=2),
+                in_=st["o", i][:].rearrange("p b (w u e) -> p u (b w) e", u=2, e=2),
             )
 
-        def qo(gi, h, i0=0, w=512):
+        def rv(j):
+            if j == 0:
+                st["ob", 7] = rt("ob", [P, 2, 2, 256], BF16, 4)
+            nc.vector.tensor_copy(
+                out=st["ob", 7][:, :, j, :].rearrange("p u (w e) -> p u w e", e=2),
+                in_=st["o", 7][:, j, :].rearrange("p (w u e) -> p u w e", u=2, e=2),
+            )
+
+        def to(i):
+            st["to", i] = turn_packed(st["ob", i][:])
+
+        def eo(i, r):
+            h, pi = divmod(i, 4)
+            gi, hf = divmod(pi, 2)
+            dst = o_t[h][:].rearrange("p i t -> p (i t)").bitcast(F32).rearrange("p (g i t u) -> p g i t u", g=2, t=4, u=2)
+            nc.scalar.copy(
+                out=dst[:, gi, r, 2 * hf : 2 * hf + 2, :],
+                in_=st["to", i][:].rearrange("p (u t i) -> p i t u", u=2, t=2)[:, r],
+            )
+
+        def qo(h, i0, w):
             r = slice(i0, i0 + w)
-            quant(o_q[h][gi][:, r], o_s[h][gi][:, r], st["ot", h][:, gi, r, :].rearrange("p i t -> p (i t)"))
+            quant(o_q[h][:, r], o_s[h][:, r], o_t[h][:, r, :].rearrange("p i t -> p (i t)"))
+
+        def sq(h, gi):
+            r = slice(512 * gi, 512 * gi + 512)
             nc.sync.dma_start(
-                out=out_1[h, :, 512 * gi + i0 : 512 * gi + i0 + w, :].rearrange("p m t -> p (m t)").bitcast(I32),
-                in_=o_q[h][gi][:, r].bitcast(I32),
+                out=out_1[h, :, r, :].rearrange("p m t -> p (m t)").bitcast(I32), in_=o_q[h][:, r].bitcast(I32)
             )
-            if i0 + w == 512:
-                for q in range(4):
-                    (nc.scalar if q % 2 else nc.sync).dma_start(
-                        out=out_2[h, 4 * q : 4 * q + 4, 512 * gi : 512 * gi + 512].bitcast(I32),
-                        in_=o_s[h][gi][32 * q : 32 * q + 4, :].bitcast(I32),
-                    )
 
-        def run(n):
-            d = [int(z) for z in n[2:] if z in "0123456789"]
-            f = n[:2]
-            table = {"tx": tx, "xp": xp, "qx": qx, "tc": tcc, "ec": ec, "mu": mu, "il": il, "qg": qg, "ki": ki, "qk": qk,
-                     "m1": m1, "nu": nu, "tn": tn, "en": en, "qn": qn, "ta": ta, "ea": ea, "qa": qa, "dg": dg, "dd": ddf,
-                     "m2": m2, "st": stt, "to": to}
-            if f in table:
-                table[f](*d)
-            elif f == "qc":
-                qc()
-            elif f == "rd":
-                if RP:
-                    rd(d[0], d[1])
-                else:
-                    rd(d[0] // 2, d[1], d[0] % 2)
-            elif f == "rv":
-                rd(3, 1, d[0] - 6)
-            elif n == "eo31":
-                eo(3, 1, slice(0, 64))
-            elif n == "fo31":
-                eo(3, 1, slice(64, 128))
-            elif f == "eo":
-                eo(d[0], d[1])
-            elif n == "qp11":
-                qo(1, 1, 0, 256)
-            elif n == "qo11":
-                qo(1, 1, 256, 256)
-            elif f == "qo":
-                qo(d[0], d[1])
+        def so(h):
+            for q in range(4):
+                (nc.scalar if h and q % 2 else nc.sync).dma_start(
+                    out=out_2[h, 4 * q : 4 * q + 4, :].bitcast(I32), in_=o_s[h][32 * q : 32 * q + 4, :].bitcast(I32)
+                )
 
+        def qo_full(h, gi):
+            qo(h, 512 * gi, 512)
+            sq(h, gi)
+            if (h, gi) == (0, 1):
+                so(0)
+
+        def qo_last(part):
+            qo(1, 512 + 256 * part, 256)
+            if part == 1:
+                sq(1, 1)
+                so(1)
+
+        for i in range(16):
+            h, ti = divmod(i, 8)
+            add("m2", lambda i=i: m2(i), ("qa", ti // 4), ("qn", ti // 4), ("qg", h), ("qk", h))
+            add("st", lambda i=i: stt(i), ("m2", i), ("dd", ti // 4))
+        for i in range(8):
+            if i < 7:
+                add("rd", lambda i=i: rd(i), ("st", 2 * i + 1))
+                add("to", lambda i=i: to(i), ("rd", i))
+                add("eo", lambda i=i: eo(i, slice(0, 128)), ("to", i))
+        for j in range(2):
+            add("rv", lambda j=j: rv(j), ("st", 14 + j))
+            if j == 0:
+                add("to", lambda: to(7), ("rv", 1))
+            add("eo", lambda j=j: eo(7, slice(64 * j, 64 * j + 64)), ("to", 7))
+        for i in range(3):
+            add("qo", lambda i=i: qo_full(i // 2, i % 2), ("eo", 2 * i + 1))
+        for j in range(2):
+            add("qo", lambda j=j: qo_last(j), ("eo", 7 + j))
+
+        queues = []
+        for text in QUEUES:
+            queue = []
+            for word in text.split():
+                parts = word.split("*")
+                queue.extend([parts[0]] * (int(parts[1]) if len(parts) > 1 else 1))
+            queues.append(queue)
+        done = dict((kind, 0) for kind in steps)
         with tc.manual_schedule():
-            for n in ORDER.split():
-                run(n)
+            while any(queues):
+                for queue in queues:
+                    if queue:
+                        kind = queue[0]
+                        action, needs = steps[kind][done[kind]]
+                        if all(done[other] > number for other, number in needs):
+                            action()
+                            done[kind] += 1
+                            queue.remove(kind)
+        assert all(done[kind] == len(steps[kind]) for kind in steps)

from contextlib import ExitStack

import concourse.mybir as mybir
from concourse.masks import make_identity

S, N, M = 1024, 1024, 512
FLOPS = 2 * S * N * M + 2 * S * M * N + 2 * S * S * N

F32 = mybir.dt.float32
BF16 = mybir.dt.bfloat16
U32 = mybir.dt.uint32
I32 = mybir.dt.int32
U8 = mybir.dt.uint8
FP8X4 = mybir.dt.float8_e4m3fn_x4
MULT = mybir.AluOpType.mult
ADD = mybir.AluOpType.add
SUB = mybir.AluOpType.subtract
COPY = mybir.ActivationFunctionType.Copy

P = 128
NS = 3
QUEUES = (
    "tx*4 tc*4 tx*4 m1*4 ta tn ta*2 m1 ta tn ta*2 m1 dg m1*2 ta*2 tn m2*2 tn dg m2*6 to*2 m2*4 to*2 m2*4 to*4",
    "xp*3 qx xp mv qx mv*2 xp qc xp mv*2 xp nu*2 xp qx nu*2 qg qx nu qk qn nu qa dd nu*2 qk st qa qn dd st*5 qg st*5 qo st*3 qo st*2 rv*2 qo*3",
    "ms*3 ec*4 il*2 ea*3 en ea en ea*2 il ea*2 en*2 il rd*3 eo rd eo rd eo*2 rd*2 eo*5",
    "ki*8",
)


def tile_signedkalmanconsensusfilterstep_x1_kernel(tc, x, y, p, c, k, a, g, out_0, out_1, out_2):
    nc = tc.nc
    with ExitStack() as ctx:
        keep = ctx.enter_context(tc.tile_pool(name="keep", bufs=1))
        ring = ctx.enter_context(tc.tile_pool(name="ring", bufs=1))
        psum_t = ctx.enter_context(tc.psum_pool(name="psum_t", bufs=4))
        psum_o = ctx.enter_context(tc.psum_pool(name="psum_o", bufs=4))

        def kt(name, shape, dtype, tag=None):
            return keep.tile(shape, dtype, name=name, tag=tag or name, align_bytes=64)

        def rt(name, shape, dtype, bufs):
            return ring.tile(shape, dtype, name=name, align_bytes=64, bufs=bufs)

        ident = kt("ident", [P, P], F32)
        p_t = kt("p_t", [P, 2, 4], BF16)
        g_t = kt("g_t", [P, 2, 4], BF16)
        hg = kt("hg", [P, 2, 4], BF16)
        hgf = kt("hgf", [P, 2, 4], F32)
        dd = kt("dd", [P, 8], F32)
        x_sb = kt("x_sb", [P, 8, N], BF16)
        a_sb = kt("a_sb", [P, 8, S], BF16)
        y_sb = kt("y_sb", [P, 8, M], BF16)
        c_sb = kt("c_sb", [P, 4, N], BF16, "w0")
        k_sb = kt("k_sb", [P, 4, N], BF16, "w1")
        c_t = kt("c_t", [P, 2, M, 4], BF16, "w2")
        k_i = kt("k_i", [P, N, 4], BF16, "w2")
        o_t = [kt("o_t%d" % h, [P, S, 4], BF16, "w%d" % h) for h in range(2)]
        xm = kt("xm", [P, 8, N], BF16)
        c_q = kt("c_q", [P, 2, M], U32)
        c_s = kt("c_s", [P, 2, M], U8)
        k_q = kt("k_q", [P, N], U32)
        k_s = kt("k_s", [P, N], U8)
        g_q = kt("g_q", [P, 2, 2, 512], U32)
        g_s = kt("g_s", [P, 2, 2, 512], U8)
        x_q = kt("x_q", [P, 4, 2, 256], U32)
        x_s = kt("x_s", [P, 4, 2, 256], U8)
        n_q = kt("n_q", [P, S], U32)
        n_s = kt("n_s", [P, S], U8)
        a_q = kt("a_q", [P, 8, 2, P], U32)
        a_s = kt("a_s", [P, 8, 2, P], U8)
        o_q = [kt("o_q%d" % h, [P, S], U32) for h in range(2)]
        o_s = [kt("o_s%d" % h, [P, S], U8) for h in range(2)]
        nt = kt("nt", [P, S, 4], BF16)
        at = kt("at", [P, 8, 2, P, 4], BF16)

        nc.scalar.dma_start(out=g_t[:], in_=g.rearrange("(h q t) -> q h t", h=2, t=4))
        nc.scalar.dma_start(out=p_t[:], in_=p.rearrange("(h q t) -> q h t", h=2, t=4))
        make_identity(nc, ident[:])
        xr = x.rearrange("(g p t) n -> g p t n", g=2, t=4)
        ar = a.rearrange("(g p t) n -> g p t n", g=2, t=4)
        yr = y.rearrange("(g p t) n -> g p t n", g=2, t=4)
        cr = c.rearrange("(b p) n -> p b n", p=P)
        kr = k.rearrange("(p t) n -> p t n", t=4)

        def load(dst, src, rows, cols):
            nc.sync.dma_start(out=dst[:, rows, cols], in_=src[:, slice(rows.start % 4, rows.start % 4 + rows.stop - rows.start), cols])

        whole, left, right = slice(0, 1024), slice(0, 512), slice(512, 1024)
        load(x_sb, xr[0], slice(0, 2), left)
        load(x_sb, xr[0], slice(0, 2), right)
        load(x_sb, xr[0], slice(2, 4), whole)
        load(c_sb, cr, slice(0, 2), whole)
        load(c_sb, cr, slice(2, 4), whole)
        load(x_sb, xr[1], slice(4, 6), whole)
        load(x_sb, xr[1], slice(6, 8), whole)
        load(y_sb, yr[0], slice(0, 4), left)
        load(k_sb, kr, slice(0, 4), left)
        load(a_sb, ar[0], slice(0, 2), whole)
        load(a_sb, ar[0], slice(2, 4), whole)
        load(k_sb, kr, slice(0, 4), right)
        load(a_sb, ar[1], slice(4, 6), whole)
        load(y_sb, yr[1], slice(4, 8), left)
        load(a_sb, ar[1], slice(6, 8), whole)
        nc.vector.tensor_scalar_mul(hgf[:], g_t[:], 0.5)
        nc.vector.tensor_scalar_mul(hg[:], g_t[:], 0.5)

        st = {}
        steps = {}

        def add(kind, action, *needs):
            steps.setdefault(kind, []).append((action, needs))

        def bank(pool, width=512):
            return pool.tile([P, width], F32, name="bank")

        def turn_rows(tiles, ng):
            ps = bank(psum_t)
            for u in range(2):
                for j in range(2):
                    words = tiles[:, j, :].bitcast(F32)
                    o = 256 * u + 128 * j
                    nc.tensor.transpose(ps[:, o : o + 128], words[:, 256 * ng + u : 256 * ng + 256 : 2], ident[:])
            return ps

        def turn_packed(src):
            ps = bank(psum_t)
            words = src.rearrange("p u b w -> p (u b w)").bitcast(F32)
            for o in range(0, 512, 128):
                nc.tensor.transpose(ps[:, o : o + 128], words[:, o : o + 128], ident[:])
            return ps

        def wout(ap):
            return ap.bitcast(F32).rearrange("p (r u) -> p r u", u=2)

        def win(ps):
            return ps[:].rearrange("p (u r) -> p r u", u=2)

        def quant(q, s, src):
            nc.vector.quantize_mx(out=q.bitcast(FP8X4), scales=s, in_=src)

        def mx(ps, lq, ls, rq, rs, first, last):
            nc.tensor.matmul_mx(
                out=ps[:], lhsT=lq.bitcast(FP8X4), lhsT_scale=ls, rhs=rq.bitcast(FP8X4), rhs_scale=rs, start=first, stop=last
            )

        def tx(i):
            pi, ng = divmod(i, 2)
            st["tx", i] = turn_rows(x_sb[:, 2 * pi : 2 * pi + 2, :], ng)

        def xp(i):
            pi, ng = divmod(i, 2)
            if ng == 0:
                st["xt", pi] = rt("xt", [P, 2, 1024], BF16, 3)
            nc.vector.tensor_tensor(
                out=st["xt", pi][:, ng, :].rearrange("p (s u e) -> p s u e", u=2, e=2),
                in0=st["tx", i][:].bitcast(BF16).rearrange("p (u s e) -> p s u e", u=2, e=2),
                in1=p_t[:, ng, :].rearrange("p (u e) -> p u e", e=2).unsqueeze(1).broadcast_to([P, 256, 2, 2]),
                op=MULT,
            )

        def qx(i):
            quant(
                x_q[:, i].rearrange("p n s -> p (n s)"), x_s[:, i].rearrange("p n s -> p (n s)"),
                st["xt", i][:].rearrange("p n s -> p (n s)"),
            )

        for i in range(8):
            add("tx", lambda i=i: tx(i))
            add("xp", lambda i=i: xp(i), ("tx", i))
        for i in range(4):
            add("qx", lambda i=i: qx(i), ("xp", 2 * i + 1))

        def tcc(i):
            b, ng = divmod(i, 2)
            st["tc", i] = turn_rows(c_sb[:, 2 * b : 2 * b + 2, :], ng)

        def ec(i):
            b, ng = divmod(i, 2)
            cols = slice(256 * b, 256 * b + 256)
            nc.scalar.copy(out=wout(c_t[:, ng, cols, :].rearrange("p m t -> p (m t)")), in_=win(st["tc", i]))

        def qc():
            quant(
                c_q[:].rearrange("p n m -> p (n m)"), c_s[:].rearrange("p n m -> p (n m)"),
                c_t[:].rearrange("p n m t -> p (n m t)"),
            )

        for i in range(4):
            add("tc", lambda i=i: tcc(i))
            add("ec", lambda i=i: ec(i), ("tc", i))
        add("qc", qc, ("ec", 3))

        def mu(ti, eng):
            gi, t = divmod(ti, 4)
            sc = hgf[:, gi, t : t + 1]
            if eng == "S":
                nc.scalar.activation(out=xm[:, ti, :], in_=x_sb[:, ti, :], func=COPY, scale=sc)
            else:
                nc.vector.tensor_scalar_mul(xm[:, ti, :], x_sb[:, ti, :], sc)

        def il(i):
            h, gi = divmod(i, 2)
            if gi == 0:
                st["xi", h] = rt("xi", [P, 2, 512, 4], BF16, 2)
            cols = slice(512 * h, 512 * h + 512)
            nc.scalar.copy(out=st["xi", h][:, gi], in_=xm[:, 4 * gi : 4 * gi + 4, cols].rearrange("p t n -> p n t"))

        def qg(h):
            quant(
                g_q[:, h].rearrange("p g n -> p (g n)"), g_s[:, h].rearrange("p g n -> p (g n)"),
                st["xi", h][:].rearrange("p g n t -> p (g n t)"),
            )

        for ti in range(NS):
            add("ms", lambda ti=ti: mu(ti, "S"))
        for ti in range(NS, 8):
            add("mv", lambda ti=ti: mu(ti, "V"))
        for i in range(4):
            add("il", lambda i=i: il(i), *((("mv", 7 - NS),) if i % 2 else (("ms", min(NS, 4) - 1), ("mv", 3 - NS))))
        for h in range(2):
            add("qg", lambda h=h: qg(h), ("il", 2 * h + 1))

        def ki(i):
            cols = slice(128 * i, 128 * i + 128)
            nc.gpsimd.tensor_scalar(
                out=k_i[:, cols, :], in0=k_sb[:, :, cols].rearrange("p t n -> p n t"),
                scalar1=1.0, scalar2=0.0, op0=MULT, op1=ADD,
            )

        def qk(h):
            cols = slice(512 * h, 512 * h + 512)
            quant(k_q[:, cols], k_s[:, cols], k_i[:, cols, :].rearrange("p n t -> p (n t)"))

        for i in range(8):
            add("ki", lambda i=i: ki(i), ("qc", 0))
        for h in range(2):
            add("qk", lambda h=h: qk(h), ("ki", 4 * h + 3))

        def m1(ti):
            pi, j = divmod(ti, 2)
            cols = slice(128 * j, 128 * j + 128)
            ps = bank(psum_o)
            for ng in range(2):
                mx(ps, x_q[:, pi, ng, cols], x_s[:, pi, ng, cols], c_q[:, ng, :], c_s[:, ng, :], ng == 0, ng == 1)
            st["m1", ti] = ps

        def nu(ti):
            if ti % 2 == 0:
                st["nu", ti // 2] = rt("nu", [P, 2, 2, 256], BF16, 3)
            nc.vector.tensor_tensor(
                out=st["nu", ti // 2][:, :, ti % 2, :].rearrange("p u (w e) -> p u w e", e=2),
                in0=y_sb[:, ti, :].rearrange("p (w u e) -> p u w e", u=2, e=2),
                in1=st["m1", ti][:].rearrange("p (w u e) -> p u w e", u=2, e=2),
                op=SUB,
            )

        def tn(pi):
            st["tn", pi] = turn_packed(st["nu", pi][:])

        def en(pi):
            rows = slice(256 * pi, 256 * pi + 256)
            nc.scalar.copy(out=wout(nt[:, rows, :].rearrange("p s t -> p (s t)")), in_=win(st["tn", pi]))

        def qn(i):
            rows = slice(512 * i, 512 * i + 512)
            quant(n_q[:, rows], n_s[:, rows], nt[:, rows, :].rearrange("p s t -> p (s t)"))

        for ti in range(8):
            add("m1", lambda ti=ti: m1(ti), ("qx", ti // 2), ("qc", 0))
            add("nu", lambda ti=ti: nu(ti), ("m1", ti))
        for pi in range(4):
            add("tn", lambda pi=pi: tn(pi), ("nu", 2 * pi + 1))
            add("en", lambda pi=pi: en(pi), ("tn", pi))
        for i in range(2):
            add("qn", lambda i=i: qn(i), ("en", 2 * i + 1))

        def ta(ti):
            ps = bank(psum_t)
            words = a_sb[:, ti, :].bitcast(F32)
            for jg in range(2):
                for u in range(2):
                    o = 256 * jg + 128 * u
                    nc.tensor.transpose(ps[:, o : o + 128], words[:, 256 * jg + u : 256 * jg + 256 : 2], ident[:])
            st["ta", ti] = ps

        def ea(ti):
            nc.scalar.copy(
                out=at[:, ti].rearrange("p j i t -> p (j i t)").bitcast(F32).rearrange("p (j i u) -> p j i u", j=2, u=2),
                in_=st["ta", ti][:].rearrange("p (j u i) -> p j i u", j=2, u=2),
            )

        def qa(i):
            tl = slice(4 * i, 4 * i + 4)
            quant(
                a_q[:, tl].rearrange("p b j i -> p (b j i)"), a_s[:, tl].rearrange("p b j i -> p (b j i)"),
                at[:, tl].rearrange("p b j i t -> p (b j i t)"),
            )

        def dg(i):
            ps = bank(psum_o, 4)
            for b in range(4):
                for jg in range(2):
                    for t in range(4):
                        nc.tensor.matmul(
                            ps[:, b : b + 1], at[:, 4 * i + b, jg, :, t], hg[:, jg, t : t + 1],
                            start=(jg == 0 and t == 0), stop=(jg == 1 and t == 3),
                        )
            st["dg", i] = ps

        def ddf(i):
            nc.vector.tensor_scalar(
                out=dd[:, 4 * i : 4 * i + 4], in0=st["dg", i][:], scalar1=-1.0, scalar2=1.0, op0=MULT, op1=ADD
            )

        for ti in range(8):
            add("ta", lambda ti=ti: ta(ti))
            add("ea", lambda ti=ti: ea(ti), ("ta", ti))
        for i in range(2):
            add("qa", lambda i=i: qa(i), ("ea", 4 * i + 3))
            add("dg", lambda i=i: dg(i), ("ea", 4 * i + 3))
            add("dd", lambda i=i: ddf(i), ("dg", i))

        def m2(i):
            h, ti = divmod(i, 8)
            ps = bank(psum_o)
            for jg in range(2):
                mx(ps, a_q[:, ti, jg, :], a_s[:, ti, jg, :], g_q[:, h, jg, :], g_s[:, h, jg, :], jg == 0, False)
            rows, cols = slice(128 * ti, 128 * ti + 128), slice(512 * h, 512 * h + 512)
            mx(ps, n_q[:, rows], n_s[:, rows], k_q[:, cols], k_s[:, cols], False, True)
            st["m2", i] = ps

        out_r = out_0.rearrange("(g p t) n -> p g t n", g=2, t=4)

        def stt(i):
            h, ti = divmod(i, 8)
            gi, t = divmod(ti, 4)
            if i % 2 == 0:
                st["o", i // 2] = rt("o", [P, 2, 512], F32, 5)
            cols = slice(512 * h, 512 * h + 512)
            o = st["o", i // 2][:, i % 2, :]
            nc.vector.scalar_tensor_tensor(
                out=o, in0=x_sb[:, ti, cols], scalar=dd[:, ti : ti + 1], in1=st["m2", i][:], op0=MULT, op1=ADD
            )
            if i % 2:
                nc.sync.dma_start(out=out_r[:, gi, t - 1 : t + 1, cols], in_=st["o", i // 2][:])

        def rd(i):
            st["ob", i] = rt("ob", [P, 2, 2, 256], BF16, 4)
            nc.scalar.copy(
                out=st["ob", i][:].rearrange("p u b (w e) -> p u (b w) e", e=2),
                in_=st["o", i][:].rearrange("p b (w u e) -> p u (b w) e", u=2, e=2),
            )

        def rv(j):
            if j == 0:
                st["ob", 7] = rt("ob", [P, 2, 2, 256], BF16, 4)
            nc.vector.tensor_copy(
                out=st["ob", 7][:, :, j, :].rearrange("p u (w e) -> p u w e", e=2),
                in_=st["o", 7][:, j, :].rearrange("p (w u e) -> p u w e", u=2, e=2),
            )

        def to(i):
            st["to", i] = turn_packed(st["ob", i][:])

        def eo(i, r):
            h, pi = divmod(i, 4)
            gi, hf = divmod(pi, 2)
            dst = o_t[h][:].rearrange("p i t -> p (i t)").bitcast(F32).rearrange("p (g i t u) -> p g i t u", g=2, t=4, u=2)
            nc.scalar.copy(
                out=dst[:, gi, r, 2 * hf : 2 * hf + 2, :],
                in_=st["to", i][:].rearrange("p (u t i) -> p i t u", u=2, t=2)[:, r],
            )

        def qo(h, i0, w):
            r = slice(i0, i0 + w)
            quant(o_q[h][:, r], o_s[h][:, r], o_t[h][:, r, :].rearrange("p i t -> p (i t)"))

        def sq(h, gi):
            r = slice(512 * gi, 512 * gi + 512)
            nc.sync.dma_start(
                out=out_1[h, :, r, :].rearrange("p m t -> p (m t)").bitcast(I32), in_=o_q[h][:, r].bitcast(I32)
            )

        def so(h):
            for q in range(4):
                (nc.scalar if h and q % 2 else nc.sync).dma_start(
                    out=out_2[h, 4 * q : 4 * q + 4, :].bitcast(I32), in_=o_s[h][32 * q : 32 * q + 4, :].bitcast(I32)
                )

        def qo_full(h, gi):
            qo(h, 512 * gi, 512)
            sq(h, gi)
            if (h, gi) == (0, 1):
                so(0)

        def qo_last(part):
            qo(1, 512 + 256 * part, 256)
            if part == 1:
                sq(1, 1)
                so(1)

        for i in range(16):
            h, ti = divmod(i, 8)
            add("m2", lambda i=i: m2(i), ("qa", ti // 4), ("qn", ti // 4), ("qg", h), ("qk", h))
            add("st", lambda i=i: stt(i), ("m2", i), ("dd", ti // 4))
        for i in range(8):
            if i < 7:
                add("rd", lambda i=i: rd(i), ("st", 2 * i + 1))
                add("to", lambda i=i: to(i), ("rd", i))
                add("eo", lambda i=i: eo(i, slice(0, 128)), ("to", i))
        for j in range(2):
            add("rv", lambda j=j: rv(j), ("st", 14 + j))
            if j == 0:
                add("to", lambda: to(7), ("rv", 1))
            add("eo", lambda j=j: eo(7, slice(64 * j, 64 * j + 64)), ("to", 7))
        for i in range(3):
            add("qo", lambda i=i: qo_full(i // 2, i % 2), ("eo", 2 * i + 1))
        for j in range(2):
            add("qo", lambda j=j: qo_last(j), ("eo", 7 + j))

        queues = []
        for text in QUEUES:
            queue = []
            for word in text.split():
                parts = word.split("*")
                queue.extend([parts[0]] * (int(parts[1]) if len(parts) > 1 else 1))
            queues.append(queue)
        done = dict((kind, 0) for kind in steps)
        with tc.manual_schedule():
            while any(queues):
                for queue in queues:
                    if queue:
                        kind = queue[0]
                        action, needs = steps[kind][done[kind]]
                        if all(done[other] > number for other, number in needs):
                            action()
                            done[kind] += 1
                            queue.remove(kind)
        assert all(done[kind] == len(steps[kind]) for kind in steps)
